import numpy as np
import ml_dtypes


def mxq(x, axis, fmt="e4m3"):
    dtype, down = {"e4m3": (ml_dtypes.float8_e4m3fn, 7), "e5m2": (ml_dtypes.float8_e5m2, 14)}[fmt]
    v = np.moveaxis(np.asarray(x, np.float32).astype(ml_dtypes.bfloat16).astype(np.float64), axis, -1)
    blocks = v.reshape(v.shape[:-1] + (-1, 32))
    amax = np.abs(blocks).max(-1, keepdims=True)
    byte = np.maximum(np.where(amax > 0, np.frexp(amax)[1] - 1 + 127, 0) - down, 1)
    scale = np.exp2(byte - 127.0)
    codes = (blocks / scale).astype(np.float32).astype(dtype).astype(np.float64)
    return np.moveaxis((codes * scale).reshape(v.shape), -1, axis)


WIDE = False


def mx_kscale(k):
    if not WIDE:
        return np.ones(k)
    levels = np.array([10, -10, 5, -5, 0])
    if k % 512:
        return np.exp2(np.random.permutation(np.resize(levels, k // 32))).repeat(32)
    a = np.empty((k // 512, 16))
    for p in range(k // 512):
        a[p, :8] = np.random.permutation(np.resize(levels, 8))
        for g in range(8):
            far = levels[np.abs(levels - a[p, g]) >= 10]
            a[p, g + 8] = far[np.random.randint(len(far))]
    return np.exp2(a.ravel()).repeat(32)


def f64(x):
    return np.asarray(x).astype(np.float64)


def striped(idx):
    return np.tile(idx.reshape(-1, 16).T, (8, 1)).astype(np.uint16)


def unstriped(offs):
    return offs[:16].T.reshape(-1).astype(np.int64)


def pack_weight(w):
    k, n = w.shape
    w = f64(np.asarray(w, np.float32).astype(ml_dtypes.bfloat16)).reshape(k // 32, 32, n)
    amax = np.abs(w).max(1)
    byte = np.clip(np.where(amax > 0, np.frexp(amax)[1] - 1 + 127 - 7, 1), 1, 254)
    scaled = (w * np.exp2(127.0 - byte)[:, None, :]).reshape(k, n).astype(np.float32)
    words = np.ascontiguousarray(scaled.reshape(k // 512, 128, 4, n).transpose(0, 1, 3, 2)).astype(ml_dtypes.float8_e4m3fn).view(np.uint8)
    return words, np.ascontiguousarray(byte.astype(np.uint8).reshape(k // 512, 16, n))


def unpack_weight(words, scales):
    g, p, n, _ = words.shape
    vals = np.ascontiguousarray(words).view(ml_dtypes.float8_e4m3fn).astype(np.float64) * np.repeat(np.exp2(scales.astype(np.float64) - 127.0), 8, axis=1)[..., None]
    return vals.transpose(0, 1, 3, 2).reshape(g * 512, n)


def relu(v):
    return np.maximum(v, 0.0)


K, T, S, H, N, U = 512, 2048, 1024, 512, 128, 1024


def setup_inputs():
    n = np.random.standard_normal
    s = mx_kscale(K)[:, None]
    u = mx_kscale(H)
    packed_w3 = pack_weight(n((H, N)) / np.sqrt(H) / u[:, None])
    return {
        "xT": (n((K, T)) * s).astype(np.float32),
        "w1": (n((K, H)) / np.sqrt(2 * K) / s * u).astype(np.float32),
        "w2": (n((K, H)) / np.sqrt(2 * K) / s * u).astype(np.float32),
        "w3_words": packed_w3[0],
        "w3_scales": packed_w3[1],
        "offs": striped(np.random.permutation(T)[:S]),
        "src": striped(np.random.permutation(S)[(S * np.random.uniform(0, 1, U) ** 4).astype(np.int64)]),
        "dst": striped(np.random.permutation(S)),
    }


def reference(xT, w1, w2, w3_words, w3_scales, offs, src, dst):
    xq = mxq(f64(xT)[:, unstriped(offs)], 0, "e4m3")
    y = mxq(f64(w1), 0, "e4m3").T @ xq
    e = mxq(f64(w2), 0, "e4m3").T @ xq
    z = relu(y[:, unstriped(src)] + e[:, unstriped(dst)])
    return unpack_weight(w3_words, w3_scales).T @ mxq(z, 0, "e4m3")

@@ -1,0 +1,183 @@
+from contextlib import ExitStack
+
+import concourse.mybir as mybir
+
+F32 = mybir.dt.float32
+BF16 = mybir.dt.bfloat16
+I32 = mybir.dt.int32
+U32 = mybir.dt.uint32
+U16 = mybir.dt.uint16
+U8 = mybir.dt.uint8
+FP8X4 = mybir.dt.float8_e4m3fn_x4
+ACT = mybir.ActivationFunctionType
+ALU = mybir.AluOpType
+
+K, T, S, H, N = 512, 2048, 1024, 512, 128
+P = 128
+PACK = 4
+FLOPS = 2 * (2 * K * H * S + H * N * S)
+
+X_CHUNKS = (512, 512, 512, 256, 256)
+EDGE_PIECES = (512, 256, 256)
+HALF = 512
+
+
+def weave(view):
+    return view.rearrange("p (c i) t -> p c t i", i=4)
+
+
+def rows(view):
+    return view.rearrange("p t (c i) -> p c t i", i=4)
+
+
+def tile_picked_hub_relu_e_kernel(
+    tc, xT, w1, w2, w3_words, w3_scales, offs, src, dst, out
+):
+    nc = tc.nc
+    with ExitStack() as ctx:
+        keep = ctx.enter_context(tc.tile_pool(name="keep", bufs=1))
+        ring = ctx.enter_context(tc.tile_pool(name="ring", bufs=3))
+        psum = ctx.enter_context(tc.psum_pool(name="psum", bufs=6))
+        psum_out = ctx.enter_context(tc.psum_pool(name="psum_out", bufs=2))
+
+        offs_sb = keep.tile([P, S // 16], U16, name="offs_sb")
+        src_sb = keep.tile([P, S // 16], U16, name="src_sb")
+        dst_sb = keep.tile([P, S // 16], U16, name="dst_sb")
+
+        x_words = keep.tile([P, T], U32, name="x_words", align_bytes=64)
+        x_bytes = keep.tile([P, T], U8, name="x_bytes", align_bytes=64)
+        w3_codes = keep.tile([P, N], U32, name="w3_codes", align_bytes=64)
+        w3_bytes = keep.tile([P, N], U8, name="w3_bytes", align_bytes=64)
+        nc.gpsimd.memset(x_bytes[:].bitcast(I32), 0)
+        nc.gpsimd.memset(w3_bytes[:].bitcast(I32), 0)
+
+        x_view = xT.rearrange("(p j) n -> p j n", j=PACK)
+        x_raw = []
+        c0 = 0
+        for i, width in enumerate(X_CHUNKS):
+            raw = keep.tile([P, PACK, width], F32, name=f"x_raw{i}")
+            nc.sync.dma_start(out=raw[:], in_=x_view[:, :, c0 : c0 + width])
+            x_raw.append((raw, c0, width))
+            c0 = c0 + width
+        nc.sync.dma_start(offs_sb[:], offs)
+        w_raw = []
+        for i, w in enumerate((w1, w2)):
+            w_view = w.rearrange("(p j) c -> p j c", j=PACK)
+            halves = []
+            for h in range(2):
+                raw = keep.tile([P, PACK, H // 2], F32, name=f"w_raw{i}{h}")
+                nc.sync.dma_start(out=raw[:], in_=w_view[:, :, h * (H // 2) : (h + 1) * (H // 2)])
+                halves.append(raw)
+            w_raw.append(halves)
+            if i == 0:
+                nc.sync.dma_start(src_sb[:], src)
+                nc.sync.dma_start(dst_sb[:], dst)
+        nc.sync.dma_start(
+            out=w3_codes[:].bitcast(I32),
+            in_=w3_words[0].rearrange("p n t -> p (n t)").bitcast(I32),
+        )
+        for q in range(4):
+            nc.sync.dma_start(
+                out=w3_bytes[32 * q : 32 * q + 4, :].bitcast(I32),
+                in_=w3_scales[0, 4 * q : 4 * q + 4, :].bitcast(I32),
+            )
+
+        for i, (raw, c0, width) in enumerate(x_raw):
+            grouped = keep.tile([P, width, PACK], BF16, name=f"x_bf{i}", align_bytes=64)
+            cut = width * 5 // 8
+            nc.vector.tensor_copy(out=weave(grouped[:, :cut, :]), in_=rows(raw[:, :, :cut]))
+            nc.scalar.activation(out=weave(grouped[:, cut:, :]), in_=rows(raw[:, :, cut:]), func=ACT.Copy)
+            nc.vector.quantize_mx(
+                out=x_words[:, c0 : c0 + width].bitcast(FP8X4),
+                scales=x_bytes[:, c0 : c0 + width],
+                in_=grouped[:].rearrange("p w j -> p (w j)"),
+            )
+
+        w_codes, w_bytes = [], []
+        for i in range(2):
+            grouped = keep.tile([P, PACK, P, PACK], BF16, name=f"w_bf{i}", align_bytes=64)
+            for h in range(2):
+                nc.scalar.activation(
+                    out=grouped[:, :, 64 * h : 64 * (h + 1), :].rearrange("p t m j -> p m j t"),
+                    in_=w_raw[i][h][:].rearrange("p j (m t) -> p m j t", t=PACK),
+                    func=ACT.Copy,
+                )
+            codes = keep.tile([P, H], U32, name=f"w_codes{i}", align_bytes=64)
+            scales = keep.tile([P, H], U8, name=f"w_bytes{i}", align_bytes=64)
+            w_codes.append(codes)
+            w_bytes.append(scales)
+            w_raw[i] = grouped
+
+        def quantise_weight(i):
+            nc.vector.quantize_mx(
+                out=w_codes[i][:].bitcast(FP8X4),
+                scales=w_bytes[i][:],
+                in_=w_raw[i][:].rearrange("p t m j -> p (t m j)"),
+            )
+
+        picked = []
+        for h in range(2):
+            cols = slice(h * HALF // 16, (h + 1) * HALF // 16)
+            words = keep.tile([P, HALF], U32, name=f"pick_words{h}", align_bytes=64)
+            scales = keep.tile([P, HALF], U8, name=f"pick_bytes{h}", align_bytes=64)
+            nc.vector.tensor_copy(words[:], x_words[:].indirect(offs_sb[:, cols]))
+            nc.vector.tensor_copy(scales[:], x_bytes[:].indirect(offs_sb[:, cols]))
+            picked.append((words, scales))
+            quantise_weight(h)
+
+        parts = [[None] * PACK, [None] * PACK]
+        for t in range(PACK):
+            for i in range(2):
+                full = keep.tile([P, S], F32, name=f"part{i}{t}")
+                parts[i][t] = full
+                for h in range(2):
+                    acc = psum.tile([P, HALF], F32, name="acc")
+                    nc.tensor.matmul_mx(
+                        out=acc[:],
+                        lhsT=w_codes[i][:, t * P : (t + 1) * P].bitcast(FP8X4),
+                        lhsT_scale=w_bytes[i][:, t * P : (t + 1) * P],
+                        rhs=picked[h][0][:].bitcast(FP8X4),
+                        rhs_scale=picked[h][1][:],
+                        start=True,
+                        stop=True,
+                    )
+                    nc.scalar.copy(out=full[:, h * HALF : (h + 1) * HALF], in_=acc[:])
+
+        r0 = 0
+        for n, width in enumerate(EDGE_PIECES):
+            cols = slice(r0 // 16, (r0 + width) // 16)
+            z = keep.tile([P, PACK, width], F32, name=f"z{n}")
+            for t in range(PACK):
+                from_src = ring.tile([P, width], F32, name="from_src")
+                nc.vector.tensor_copy(from_src[:], parts[0][t][:].indirect(src_sb[:, cols]))
+                nc.vector.tensor_tensor(z[:, t, :], parts[1][t][:].indirect(dst_sb[:, cols]), from_src[:], ALU.add)
+            grouped = keep.tile([P, width, PACK], BF16, name=f"z_bf{n}", align_bytes=64)
+            if n == len(EDGE_PIECES) - 1:
+                cut = width * 5 // 8
+                nc.vector.tensor_scalar(
+                    out=weave(grouped[:, :cut, :]), in0=rows(z[:, :, :cut]), scalar1=0.0, scalar2=None, op0=ALU.max
+                )
+                nc.scalar.activation(out=weave(grouped[:, cut:, :]), in_=rows(z[:, :, cut:]), func=ACT.Relu)
+            else:
+                nc.scalar.activation(out=weave(grouped[:]), in_=rows(z[:]), func=ACT.Relu)
+            z_codes = keep.tile([P, width], U32, name=f"z_codes{n}", align_bytes=64)
+            z_bytes = keep.tile([P, width], U8, name=f"z_bytes{n}", align_bytes=64)
+            nc.vector.quantize_mx(
+                out=z_codes[:].bitcast(FP8X4),
+                scales=z_bytes[:],
+                in_=grouped[:].rearrange("p w j -> p (w j)"),
+            )
+            acc = psum_out.tile([P, width], F32, name="acc_out")
+            nc.tensor.matmul_mx(
+                out=acc[:],
+                lhsT=w3_codes[:].bitcast(FP8X4),
+                lhsT_scale=w3_bytes[:],
+                rhs=z_codes[:].bitcast(FP8X4),
+                rhs_scale=z_bytes[:],
+                start=True,
+                stop=True,
+            )
+            result = keep.tile([P, width], F32, name=f"result{n}")
+            nc.scalar.copy(out=result[:], in_=acc[:])
+            nc.sync.dma_start(out=out[:, r0 : r0 + width], in_=result[:])
+            r0 = r0 + width

@@ -17,8 +17,8 @@ P = 128
 PACK = 4
 FLOPS = 2 * (2 * K * H * S + H * N * S)
 
-X_CHUNKS = (512, 512, 512, 256, 256)
-EDGE_PIECES = (512, 256, 256)
+X_CHUNKS = (((1024, 640), (1024, 704)), ((1024, 384), (512, 320), (512, 320)))
+EDGE_PIECES = (256, 256, 256, 128, 128)
 HALF = 512
 
 
@@ -36,42 +36,35 @@ def tile_picked_hub_relu_e_kernel(
     nc = tc.nc
     with ExitStack() as ctx:
         keep = ctx.enter_context(tc.tile_pool(name="keep", bufs=1))
-        ring = ctx.enter_context(tc.tile_pool(name="ring", bufs=3))
-        psum = ctx.enter_context(tc.psum_pool(name="psum", bufs=6))
-        psum_out = ctx.enter_context(tc.psum_pool(name="psum_out", bufs=2))
+        psum = ctx.enter_context(tc.psum_pool(name="psum", bufs=5))
+        psum_out = ctx.enter_context(tc.psum_pool(name="psum_out", bufs=3))
 
         offs_sb = keep.tile([P, S // 16], U16, name="offs_sb")
         src_sb = keep.tile([P, S // 16], U16, name="src_sb")
         dst_sb = keep.tile([P, S // 16], U16, name="dst_sb")
 
-        x_words = keep.tile([P, T], U32, name="x_words", align_bytes=64)
-        x_bytes = keep.tile([P, T], U8, name="x_bytes", align_bytes=64)
         w3_codes = keep.tile([P, N], U32, name="w3_codes", align_bytes=64)
         w3_bytes = keep.tile([P, N], U8, name="w3_bytes", align_bytes=64)
-        nc.gpsimd.memset(x_bytes[:].bitcast(I32), 0)
-        nc.gpsimd.memset(w3_bytes[:].bitcast(I32), 0)
+        nc.vector.memset(w3_bytes[:].bitcast(I32), 0)
 
         x_view = xT.rearrange("(p j) n -> p j n", j=PACK)
         x_raw = []
-        c0 = 0
-        for i, width in enumerate(X_CHUNKS):
-            raw = keep.tile([P, PACK, width], F32, name=f"x_raw{i}")
-            nc.sync.dma_start(out=raw[:], in_=x_view[:, :, c0 : c0 + width])
-            x_raw.append((raw, c0, width))
-            c0 = c0 + width
-        nc.sync.dma_start(offs_sb[:], offs)
+        for u, chunks in enumerate(X_CHUNKS):
+            c0 = 0
+            for i, (width, cut) in enumerate(chunks):
+                raw = keep.tile([P, 2, width], F32, name=f"x_raw{u}{i}")
+                nc.sync.dma_start(out=raw[:], in_=x_view[:, 2 * u : 2 * u + 2, c0 : c0 + width])
+                x_raw.append((u, raw, c0, width, cut))
+                c0 = c0 + width
+            if u == 0:
+                nc.sync.dma_start(offs_sb[:], offs)
         w_raw = []
         for i, w in enumerate((w1, w2)):
-            w_view = w.rearrange("(p j) c -> p j c", j=PACK)
-            halves = []
-            for h in range(2):
-                raw = keep.tile([P, PACK, H // 2], F32, name=f"w_raw{i}{h}")
-                nc.sync.dma_start(out=raw[:], in_=w_view[:, :, h * (H // 2) : (h + 1) * (H // 2)])
-                halves.append(raw)
-            w_raw.append(halves)
-            if i == 0:
-                nc.sync.dma_start(src_sb[:], src)
-                nc.sync.dma_start(dst_sb[:], dst)
+            raw = keep.tile([P, PACK, H], F32, name=f"w_raw{i}")
+            nc.sync.dma_start(out=raw[:], in_=w.rearrange("(p j) c -> p j c", j=PACK))
+            w_raw.append(raw)
+        nc.sync.dma_start(src_sb[:], src)
+        nc.sync.dma_start(dst_sb[:], dst)
         nc.sync.dma_start(
             out=w3_codes[:].bitcast(I32),
             in_=w3_words[0].rearrange("p n t -> p (n t)").bitcast(I32),
@@ -82,94 +75,127 @@ def tile_picked_hub_relu_e_kernel(
                 in_=w3_scales[0, 4 * q : 4 * q + 4, :].bitcast(I32),
             )
 
-        for i, (raw, c0, width) in enumerate(x_raw):
-            grouped = keep.tile([P, width, PACK], BF16, name=f"x_bf{i}", align_bytes=64)
-            cut = width * 5 // 8
-            nc.vector.tensor_copy(out=weave(grouped[:, :cut, :]), in_=rows(raw[:, :, :cut]))
-            nc.scalar.activation(out=weave(grouped[:, cut:, :]), in_=rows(raw[:, :, cut:]), func=ACT.Copy)
-            nc.vector.quantize_mx(
-                out=x_words[:, c0 : c0 + width].bitcast(FP8X4),
-                scales=x_bytes[:, c0 : c0 + width],
-                in_=grouped[:].rearrange("p w j -> p (w j)"),
-            )
-
-        w_codes, w_bytes = [], []
-        for i in range(2):
-            grouped = keep.tile([P, PACK, P, PACK], BF16, name=f"w_bf{i}", align_bytes=64)
-            for h in range(2):
-                nc.scalar.activation(
-                    out=grouped[:, :, 64 * h : 64 * (h + 1), :].rearrange("p t m j -> p m j t"),
-                    in_=w_raw[i][h][:].rearrange("p j (m t) -> p m j t", t=PACK),
-                    func=ACT.Copy,
-                )
-            codes = keep.tile([P, H], U32, name=f"w_codes{i}", align_bytes=64)
-            scales = keep.tile([P, H], U8, name=f"w_bytes{i}", align_bytes=64)
-            w_codes.append(codes)
-            w_bytes.append(scales)
-            w_raw[i] = grouped
-
-        def quantise_weight(i):
-            nc.vector.quantize_mx(
-                out=w_codes[i][:].bitcast(FP8X4),
-                scales=w_bytes[i][:],
-                in_=w_raw[i][:].rearrange("p t m j -> p (t m j)"),
-            )
-
-        picked = []
-        for h in range(2):
-            cols = slice(h * HALF // 16, (h + 1) * HALF // 16)
-            words = keep.tile([P, HALF], U32, name=f"pick_words{h}", align_bytes=64)
-            scales = keep.tile([P, HALF], U8, name=f"pick_bytes{h}", align_bytes=64)
-            nc.vector.tensor_copy(words[:], x_words[:].indirect(offs_sb[:, cols]))
-            nc.vector.tensor_copy(scales[:], x_bytes[:].indirect(offs_sb[:, cols]))
-            picked.append((words, scales))
-            quantise_weight(h)
-
-        parts = [[None] * PACK, [None] * PACK]
-        for t in range(PACK):
-            for i in range(2):
-                full = keep.tile([P, S], F32, name=f"part{i}{t}")
-                parts[i][t] = full
-                for h in range(2):
-                    acc = psum.tile([P, HALF], F32, name="acc")
-                    nc.tensor.matmul_mx(
-                        out=acc[:],
-                        lhsT=w_codes[i][:, t * P : (t + 1) * P].bitcast(FP8X4),
-                        lhsT_scale=w_bytes[i][:, t * P : (t + 1) * P],
-                        rhs=picked[h][0][:].bitcast(FP8X4),
-                        rhs_scale=picked[h][1][:],
-                        start=True,
-                        stop=True,
+        pairs = [keep.tile([P, 2 * T], BF16, name=f"pairs{u}") for u in range(2)]
+        gathered = [keep.tile([P, 2, HALF], U32, name=f"gathered{h}") for h in range(2)]
+        for u in range(2):
+            view = pairs[u][:].rearrange("p (c e) -> p c e", e=2)
+            for v, raw, c0, width, cut in x_raw:
+                if v == u:
+                    nc.scalar.activation(
+                        out=view[:, c0 + cut : c0 + width, :],
+                        in_=raw[:, :, cut:].rearrange("p e c -> p c e"),
+                        func=ACT.Copy,
                     )
-                    nc.scalar.copy(out=full[:, h * HALF : (h + 1) * HALF], in_=acc[:])
+                    nc.vector.tensor_copy(
+                        out=view[:, c0 : c0 + cut, :], in_=raw[:, :, :cut].rearrange("p e c -> p c e")
+                    )
+            runs = ((0, 0, 512), (1, 0, 512)) if u == 0 else ((0, 0, 512), (1, 0, 256), (1, 256, 512))
+            for h, a, b in runs:
+                cols = slice((h * HALF + a) // 16, (h * HALF + b) // 16)
+                nc.vector.tensor_copy(gathered[h][:, u, a:b], pairs[u][:].bitcast(U32).indirect(offs_sb[:, cols]))
+        woven = [keep.tile([P, PACK * HALF], BF16, name=f"woven{h}", align_bytes=64) for h in range(2)]
+        nc.scalar.copy(
+            out=woven[0][:].bitcast(U32).rearrange("p (c u) -> p c u", u=2),
+            in_=gathered[0][:].rearrange("p u c -> p c u"),
+        )
+        for a in (0, 256):
+            nc.vector.tensor_copy(
+                out=woven[1][:].bitcast(I32).rearrange("p (c u) -> p c u", u=2)[:, a : a + 256, :],
+                in_=gathered[1][:].bitcast(I32).rearrange("p u c -> p c u")[:, a : a + 256, :],
+            )
 
-        r0 = 0
-        for n, width in enumerate(EDGE_PIECES):
-            cols = slice(r0 // 16, (r0 + width) // 16)
-            z = keep.tile([P, PACK, width], F32, name=f"z{n}")
-            for t in range(PACK):
-                from_src = ring.tile([P, width], F32, name="from_src")
-                nc.vector.tensor_copy(from_src[:], parts[0][t][:].indirect(src_sb[:, cols]))
-                nc.vector.tensor_tensor(z[:, t, :], parts[1][t][:].indirect(dst_sb[:, cols]), from_src[:], ALU.add)
+        w_codes, w_bytes = {}, {}
+
+        def prepare_weight(i, u):
+            grouped = keep.tile([P, 2, P, PACK], BF16, name=f"w_bf{i}{u}", tag=f"w_bf{i}{u}", align_bytes=64)
+            nc.scalar.activation(
+                out=grouped[:].rearrange("p t m j -> p m j t"),
+                in_=w_raw[i][:].rearrange("p j (m t) -> p m j t", t=PACK)[:, :, :, 2 * u : 2 * u + 2],
+                func=ACT.Copy,
+            )
+            w_codes[i, u] = keep.tile([P, 2 * P], U32, name=f"w_codes{i}{u}", align_bytes=64)
+            w_bytes[i, u] = keep.tile([P, 2 * P], U8, name=f"w_bytes{i}{u}", align_bytes=64)
+            nc.vector.quantize_mx(
+                out=w_codes[i, u][:].bitcast(FP8X4),
+                scales=w_bytes[i, u][:],
+                in_=grouped[:].rearrange("p t m j -> p (t m j)"),
+            )
+
+        def quantise_picked(h, words, scales, a, b):
+            nc.vector.quantize_mx(
+                out=words[:, a:b].bitcast(FP8X4), scales=scales[:, a:b], in_=woven[h][:, PACK * a : PACK * b]
+            )
+
+        words0 = keep.tile([P, HALF], U32, name="pick_words0", align_bytes=64)
+        bytes0 = keep.tile([P, HALF], U8, name="pick_bytes0", align_bytes=64)
+        quantise_picked(0, words0, bytes0, 0, HALF)
+        prepare_weight(0, 0)
+        words1 = keep.tile([P, HALF], U32, name="pick_words1", tag="w_bf00", align_bytes=64)
+        bytes1 = keep.tile([P, HALF], U8, name="pick_bytes1", align_bytes=64)
+        quantise_picked(1, words1, bytes1, 0, HALF // 2)
+        quantise_picked(1, words1, bytes1, HALF // 2, HALF)
+        prepare_weight(0, 1)
+        picked = [(words0, bytes0), (words1, bytes1)]
+
+        parts = [[keep.tile([P, S], F32, name=f"part{i}{t}") for t in range(PACK)] for i in range(2)]
+
+        def product(i, t, h, a, b, copy_out):
+            acc = psum.tile([P, b - a], F32, name="acc")
+            cols = slice((t % 2) * P, (t % 2 + 1) * P)
+            nc.tensor.matmul_mx(
+                out=acc[:],
+                lhsT=w_codes[i, t // 2][:, cols].bitcast(FP8X4),
+                lhsT_scale=w_bytes[i, t // 2][:, cols],
+                rhs=picked[h][0][:, a:b].bitcast(FP8X4),
+                rhs_scale=picked[h][1][:, a:b],
+                start=True,
+                stop=True,
+            )
+            copy_out(out=parts[i][t][:, h * HALF + a : h * HALF + b], in_=acc[:])
+
+        product(0, 0, 0, 0, HALF, nc.scalar.copy)
+        product(0, 0, 1, 0, HALF // 2, nc.scalar.copy)
+        product(0, 0, 1, HALF // 2, HALF, nc.vector.tensor_copy)
+        prepare_weight(1, 0)
+        for i, t in ((0, 1), (0, 2), (1, 0), (1, 1), (0, 3), (1, 2), (1, 3)):
+            if (i, t) == (1, 1):
+                prepare_weight(1, 1)
+            for h in range(2):
+                product(i, t, h, 0, HALF, nc.scalar.copy)
+
+        starts = [sum(EDGE_PIECES[:n]) for n in range(len(EDGE_PIECES))]
+        z = {}
+        rounded = {}
+
+        def fetch_source(t, a, b, into):
+            nc.vector.tensor_copy(into, parts[0][t][:].indirect(src_sb[:, a // 16 : b // 16]))
+
+        def add_target(t, a, b, into, fetched):
+            targets = parts[1][t][:].indirect(dst_sb[:, a // 16 : b // 16])
+            nc.vector.tensor_tensor(into, targets, fetched, ALU.add)
+
+        def rectify(n):
+            width = EDGE_PIECES[n]
             grouped = keep.tile([P, width, PACK], BF16, name=f"z_bf{n}", align_bytes=64)
             if n == len(EDGE_PIECES) - 1:
-                cut = width * 5 // 8
                 nc.vector.tensor_scalar(
-                    out=weave(grouped[:, :cut, :]), in0=rows(z[:, :, :cut]), scalar1=0.0, scalar2=None, op0=ALU.max
+                    out=weave(grouped[:]), in0=rows(z[n]), scalar1=0.0, scalar2=None, op0=ALU.max
                 )
-                nc.scalar.activation(out=weave(grouped[:, cut:, :]), in_=rows(z[:, :, cut:]), func=ACT.Relu)
             else:
-                nc.scalar.activation(out=weave(grouped[:]), in_=rows(z[:]), func=ACT.Relu)
+                nc.scalar.activation(out=weave(grouped[:]), in_=rows(z[n]), func=ACT.Relu)
+            rounded[n] = grouped
+
+        def second_product(n, acc):
+            width = EDGE_PIECES[n]
             z_codes = keep.tile([P, width], U32, name=f"z_codes{n}", align_bytes=64)
             z_bytes = keep.tile([P, width], U8, name=f"z_bytes{n}", align_bytes=64)
             nc.vector.quantize_mx(
                 out=z_codes[:].bitcast(FP8X4),
                 scales=z_bytes[:],
-                in_=grouped[:].rearrange("p w j -> p (w j)"),
+                in_=rounded[n][:].rearrange("p w j -> p (w j)"),
             )
-            acc = psum_out.tile([P, width], F32, name="acc_out")
             nc.tensor.matmul_mx(
-                out=acc[:],
+                out=acc,
                 lhsT=w3_codes[:].bitcast(FP8X4),
                 lhsT_scale=w3_bytes[:],
                 rhs=z_codes[:].bitcast(FP8X4),
@@ -177,7 +203,64 @@ def tile_picked_hub_relu_e_kernel(
                 start=True,
                 stop=True,
             )
-            result = keep.tile([P, width], F32, name=f"result{n}")
-            nc.scalar.copy(out=result[:], in_=acc[:])
-            nc.sync.dma_start(out=out[:, r0 : r0 + width], in_=result[:])
-            r0 = r0 + width
+
+        def finish(copy_out, *pieces):
+            width = sum(EDGE_PIECES[n] for n in pieces)
+            a = starts[pieces[0]]
+            acc = psum_out.tile([P, width], F32, name="acc_out")
+            for n in pieces:
+                second_product(n, acc[:, starts[n] - a : starts[n] - a + EDGE_PIECES[n]])
+            result = keep.tile([P, width], F32, name=f"result{pieces[0]}")
+            copy_out(out=result[:], in_=acc[:])
+            nc.sync.dma_start(out=out[:, a : a + width], in_=result[:])
+
+        Q = 256
+        wide = keep.tile([P, PACK, HALF], F32, name="wide", tag="wide")
+        z[0], z[1] = wide[:, :, :Q], wide[:, :, Q:]
+        for n in range(2, len(EDGE_PIECES)):
+            z[n] = keep.tile([P, PACK, EDGE_PIECES[n]], F32, name=f"z{n}")[:]
+        first = keep.tile([P, S], F32, name="first")
+        turn_a = keep.tile([P, HALF], F32, name="turn_a")
+        turn_b = keep.tile([P, HALF], F32, name="turn_b")
+        turn_c = keep.tile([P, HALF], F32, name="turn_c")
+        low, high = turn_c[:, :Q], turn_c[:, Q:]
+
+        fetch_source(0, 0, 512, first[:, :512])
+        fetch_source(0, 512, 1024, first[:, 512:])
+        fetch_source(1, 0, 512, turn_a[:])
+        fetch_source(2, 0, 512, turn_b[:])
+        add_target(0, 0, HALF, wide[:, 0, :], first[:, :HALF])
+        for n in range(2, len(EDGE_PIECES)):
+            a, b = starts[n], starts[n] + EDGE_PIECES[n]
+            add_target(0, a, b, z[n][:, 0, :], first[:, a:b])
+        add_target(1, 0, 512, wide[:, 1, :], turn_a[:])
+        fetch_source(3, 0, 512, turn_c[:])
+        add_target(2, 0, 512, wide[:, 2, :], turn_b[:])
+        add_target(3, 0, Q, z[0][:, 3, :], low)
+        rectify(0)
+        finish(nc.scalar.copy, 0)
+        add_target(3, Q, 512, z[1][:, 3, :], high)
+        rectify(1)
+        finish(nc.scalar.copy, 1)
+        fetch_source(1, 512, 768, low)
+        fetch_source(2, 512, 768, high)
+        add_target(1, 512, 768, z[2][:, 1, :], low)
+        add_target(2, 512, 768, z[2][:, 2, :], high)
+        fetch_source(3, 512, 768, low)
+        fetch_source(1, 768, 1024, high)
+        add_target(3, 512, 768, z[2][:, 3, :], low)
+        rectify(2)
+        add_target(1, 768, 896, z[3][:, 1, :], high[:, :128])
+        fetch_source(2, 768, 1024, low)
+        last = keep.tile([P, Q], F32, name="last", tag="wide")
+        fetch_source(3, 768, 1024, last[:])
+        add_target(2, 768, 896, z[3][:, 2, :], low[:, :128])
+        add_target(3, 768, 896, z[3][:, 3, :], last[:, :128])
+        rectify(3)
+        add_target(1, 896, 1024, z[4][:, 1, :], high[:, 128:])
+        add_target(2, 896, 1024, z[4][:, 2, :], low[:, 128:])
+        add_target(3, 896, 1024, z[4][:, 3, :], last[:, 128:])
+        finish(nc.scalar.copy, 2)
+        rectify(4)
+        finish(nc.scalar.copy, 3)
+        finish(nc.vector.tensor_copy, 4)

@@ -15,19 +15,26 @@ ALU = mybir.AluOpType
 K, T, S, H, N = 512, 2048, 1024, 512, 128
 P = 128
 PACK = 4
+HALF = S // 2
+QUARTER = S // 4
+EIGHTH = S // 8
 FLOPS = 2 * (2 * K * H * S + H * N * S)
 
-X_CHUNKS = (((1024, 640), (1024, 704)), ((1024, 384), (512, 320), (512, 320)))
-EDGE_PIECES = (256, 256, 256, 128, 128)
-HALF = 512
+X_LOADS = (((1024, 640), (1024, 704)), ((1024, 384), (512, 320), (512, 320)))
+
+EDGE_PIECES = (QUARTER, QUARTER, QUARTER, EIGHTH, EIGHTH)
 
 
-def weave(view):
+def interleaved(view):
     return view.rearrange("p (c i) t -> p c t i", i=4)
 
 
-def rows(view):
+def stacked(view):
     return view.rearrange("p t (c i) -> p c t i", i=4)
+
+
+def entries(offsets, a, b):
+    return offsets[:, a // 16 : b // 16]
 
 
 def tile_picked_hub_relu_e_kernel(
@@ -48,13 +55,13 @@ def tile_picked_hub_relu_e_kernel(
         nc.vector.memset(w3_bytes[:].bitcast(I32), 0)
 
         x_view = xT.rearrange("(p j) n -> p j n", j=PACK)
-        x_raw = []
-        for u, chunks in enumerate(X_CHUNKS):
+        x_raw = [[], []]
+        for u, loads in enumerate(X_LOADS):
             c0 = 0
-            for i, (width, cut) in enumerate(chunks):
+            for i, (width, cut) in enumerate(loads):
                 raw = keep.tile([P, 2, width], F32, name=f"x_raw{u}{i}")
                 nc.sync.dma_start(out=raw[:], in_=x_view[:, 2 * u : 2 * u + 2, c0 : c0 + width])
-                x_raw.append((u, raw, c0, width, cut))
+                x_raw[u].append((raw, c0, width, cut))
                 c0 = c0 + width
             if u == 0:
                 nc.sync.dma_start(offs_sb[:], offs)
@@ -79,123 +86,127 @@ def tile_picked_hub_relu_e_kernel(
         gathered = [keep.tile([P, 2, HALF], U32, name=f"gathered{h}") for h in range(2)]
         for u in range(2):
             view = pairs[u][:].rearrange("p (c e) -> p c e", e=2)
-            for v, raw, c0, width, cut in x_raw:
-                if v == u:
-                    nc.scalar.activation(
-                        out=view[:, c0 + cut : c0 + width, :],
-                        in_=raw[:, :, cut:].rearrange("p e c -> p c e"),
-                        func=ACT.Copy,
-                    )
-                    nc.vector.tensor_copy(
-                        out=view[:, c0 : c0 + cut, :], in_=raw[:, :, :cut].rearrange("p e c -> p c e")
-                    )
-            runs = ((0, 0, 512), (1, 0, 512)) if u == 0 else ((0, 0, 512), (1, 0, 256), (1, 256, 512))
-            for h, a, b in runs:
-                cols = slice((h * HALF + a) // 16, (h * HALF + b) // 16)
-                nc.vector.tensor_copy(gathered[h][:, u, a:b], pairs[u][:].bitcast(U32).indirect(offs_sb[:, cols]))
+            for raw, c0, width, cut in x_raw[u]:
+                nc.scalar.activation(
+                    out=view[:, c0 + cut : c0 + width, :],
+                    in_=raw[:, :, cut:].rearrange("p e c -> p c e"),
+                    func=ACT.Copy,
+                )
+                nc.vector.tensor_copy(out=view[:, c0 : c0 + cut, :], in_=raw[:, :, :cut].rearrange("p e c -> p c e"))
+            second_half = ((1, 0, HALF),) if u == 0 else ((1, 0, QUARTER), (1, QUARTER, HALF))
+            for h, a, b in ((0, 0, HALF),) + second_half:
+                picked_words = pairs[u][:].bitcast(U32).indirect(entries(offs_sb, h * HALF + a, h * HALF + b))
+                nc.vector.tensor_copy(gathered[h][:, u, a:b], picked_words)
+
         woven = [keep.tile([P, PACK * HALF], BF16, name=f"woven{h}", align_bytes=64) for h in range(2)]
         nc.scalar.copy(
             out=woven[0][:].bitcast(U32).rearrange("p (c u) -> p c u", u=2),
             in_=gathered[0][:].rearrange("p u c -> p c u"),
         )
-        for a in (0, 256):
+        for a in (0, QUARTER):
             nc.vector.tensor_copy(
-                out=woven[1][:].bitcast(I32).rearrange("p (c u) -> p c u", u=2)[:, a : a + 256, :],
-                in_=gathered[1][:].bitcast(I32).rearrange("p u c -> p c u")[:, a : a + 256, :],
+                out=woven[1][:].bitcast(I32).rearrange("p (c u) -> p c u", u=2)[:, a : a + QUARTER, :],
+                in_=gathered[1][:].bitcast(I32).rearrange("p u c -> p c u")[:, a : a + QUARTER, :],
             )
 
-        w_codes, w_bytes = {}, {}
+        w_rounded, w_codes, w_bytes = {}, {}, {}
 
-        def prepare_weight(i, u):
-            grouped = keep.tile([P, 2, P, PACK], BF16, name=f"w_bf{i}{u}", tag=f"w_bf{i}{u}", align_bytes=64)
-            nc.scalar.activation(
-                out=grouped[:].rearrange("p t m j -> p m j t"),
-                in_=w_raw[i][:].rearrange("p j (m t) -> p m j t", t=PACK)[:, :, :, 2 * u : 2 * u + 2],
-                func=ACT.Copy,
+        def round_weight(i, g, copy):
+            w_rounded[i, g] = keep.tile([P, 2, P, PACK], BF16, name=f"w_bf{i}{g}", tag=f"w_bf{i}{g}", align_bytes=64)
+            copy(
+                out=w_rounded[i, g][:].rearrange("p t m j -> p m j t"),
+                in_=w_raw[i][:].rearrange("p j (m t) -> p m j t", t=PACK)[:, :, :, 2 * g : 2 * g + 2],
             )
-            w_codes[i, u] = keep.tile([P, 2 * P], U32, name=f"w_codes{i}{u}", align_bytes=64)
-            w_bytes[i, u] = keep.tile([P, 2 * P], U8, name=f"w_bytes{i}{u}", align_bytes=64)
+
+        def quantise_weight(i, g):
+            w_codes[i, g] = keep.tile([P, 2 * P], U32, name=f"w_codes{i}{g}", align_bytes=64)
+            w_bytes[i, g] = keep.tile([P, 2 * P], U8, name=f"w_bytes{i}{g}", align_bytes=64)
             nc.vector.quantize_mx(
-                out=w_codes[i, u][:].bitcast(FP8X4),
-                scales=w_bytes[i, u][:],
-                in_=grouped[:].rearrange("p t m j -> p (t m j)"),
+                out=w_codes[i, g][:].bitcast(FP8X4),
+                scales=w_bytes[i, g][:],
+                in_=w_rounded[i, g][:].rearrange("p t m j -> p (t m j)"),
             )
 
-        def quantise_picked(h, words, scales, a, b):
+        x_codes, x_bytes = {}, {}
+
+        def quantise_picked(h, a, b):
             nc.vector.quantize_mx(
-                out=words[:, a:b].bitcast(FP8X4), scales=scales[:, a:b], in_=woven[h][:, PACK * a : PACK * b]
+                out=x_codes[h][:, a:b].bitcast(FP8X4), scales=x_bytes[h][:, a:b], in_=woven[h][:, PACK * a : PACK * b]
             )
 
-        words0 = keep.tile([P, HALF], U32, name="pick_words0", align_bytes=64)
-        bytes0 = keep.tile([P, HALF], U8, name="pick_bytes0", align_bytes=64)
-        quantise_picked(0, words0, bytes0, 0, HALF)
-        prepare_weight(0, 0)
-        words1 = keep.tile([P, HALF], U32, name="pick_words1", tag="w_bf00", align_bytes=64)
-        bytes1 = keep.tile([P, HALF], U8, name="pick_bytes1", align_bytes=64)
-        quantise_picked(1, words1, bytes1, 0, HALF // 2)
-        quantise_picked(1, words1, bytes1, HALF // 2, HALF)
-        prepare_weight(0, 1)
-        picked = [(words0, bytes0), (words1, bytes1)]
+        x_codes[0] = keep.tile([P, HALF], U32, name="x_codes0", align_bytes=64)
+        x_bytes[0] = keep.tile([P, HALF], U8, name="x_bytes0", align_bytes=64)
+        quantise_picked(0, 0, HALF)
+        round_weight(0, 0, nc.scalar.copy)
+        quantise_weight(0, 0)
+        x_codes[1] = keep.tile([P, HALF], U32, name="x_codes1", tag="w_bf00", align_bytes=64)
+        x_bytes[1] = keep.tile([P, HALF], U8, name="x_bytes1", align_bytes=64)
+        quantise_picked(1, 0, QUARTER)
+        quantise_picked(1, QUARTER, HALF)
+        round_weight(0, 1, nc.scalar.copy)
+        quantise_weight(0, 1)
+        round_weight(1, 0, nc.vector.tensor_copy)
 
         parts = [[keep.tile([P, S], F32, name=f"part{i}{t}") for t in range(PACK)] for i in range(2)]
 
-        def product(i, t, h, a, b, copy_out):
+        def first_product(i, t, h, a, b, copy):
             acc = psum.tile([P, b - a], F32, name="acc")
-            cols = slice((t % 2) * P, (t % 2 + 1) * P)
+            w_cols = slice((t % 2) * P, (t % 2 + 1) * P)
             nc.tensor.matmul_mx(
                 out=acc[:],
-                lhsT=w_codes[i, t // 2][:, cols].bitcast(FP8X4),
-                lhsT_scale=w_bytes[i, t // 2][:, cols],
-                rhs=picked[h][0][:, a:b].bitcast(FP8X4),
-                rhs_scale=picked[h][1][:, a:b],
+                lhsT=w_codes[i, t // 2][:, w_cols].bitcast(FP8X4),
+                lhsT_scale=w_bytes[i, t // 2][:, w_cols],
+                rhs=x_codes[h][:, a:b].bitcast(FP8X4),
+                rhs_scale=x_bytes[h][:, a:b],
                 start=True,
                 stop=True,
             )
-            copy_out(out=parts[i][t][:, h * HALF + a : h * HALF + b], in_=acc[:])
+            copy(out=parts[i][t][:, h * HALF + a : h * HALF + b], in_=acc[:])
 
-        product(0, 0, 0, 0, HALF, nc.scalar.copy)
-        product(0, 0, 1, 0, HALF // 2, nc.scalar.copy)
-        product(0, 0, 1, HALF // 2, HALF, nc.vector.tensor_copy)
-        prepare_weight(1, 0)
-        for i, t in ((0, 1), (0, 2), (1, 0), (1, 1), (0, 3), (1, 2), (1, 3)):
-            if (i, t) == (1, 1):
-                prepare_weight(1, 1)
-            for h in range(2):
-                product(i, t, h, 0, HALF, nc.scalar.copy)
+        def whole_tiles(*tiles):
+            for i, t in tiles:
+                for h in range(2):
+                    first_product(i, t, h, 0, HALF, nc.scalar.copy)
+
+        first_product(0, 0, 0, 0, HALF, nc.scalar.copy)
+        first_product(0, 0, 1, 0, QUARTER, nc.scalar.copy)
+        first_product(0, 0, 1, QUARTER, HALF, nc.vector.tensor_copy)
+        quantise_weight(1, 0)
+        whole_tiles((0, 1), (0, 2), (1, 0))
+        round_weight(1, 1, nc.scalar.copy)
+        quantise_weight(1, 1)
+        whole_tiles((1, 1), (0, 3), (1, 2), (1, 3))
 
         starts = [sum(EDGE_PIECES[:n]) for n in range(len(EDGE_PIECES))]
-        z = {}
-        rounded = {}
+        z_rounded = {}
 
         def fetch_source(t, a, b, into):
-            nc.vector.tensor_copy(into, parts[0][t][:].indirect(src_sb[:, a // 16 : b // 16]))
+            nc.vector.tensor_copy(into, parts[0][t][:].indirect(entries(src_sb, a, b)))
 
         def add_target(t, a, b, into, fetched):
-            targets = parts[1][t][:].indirect(dst_sb[:, a // 16 : b // 16])
-            nc.vector.tensor_tensor(into, targets, fetched, ALU.add)
+            nc.vector.tensor_tensor(into, parts[1][t][:].indirect(entries(dst_sb, a, b)), fetched, ALU.add)
 
-        def rectify(n):
-            width = EDGE_PIECES[n]
-            grouped = keep.tile([P, width, PACK], BF16, name=f"z_bf{n}", align_bytes=64)
+        def rectify(n, sums):
+            z_rounded[n] = keep.tile([P, EDGE_PIECES[n], PACK], BF16, name=f"z_bf{n}", align_bytes=64)
             if n == len(EDGE_PIECES) - 1:
                 nc.vector.tensor_scalar(
-                    out=weave(grouped[:]), in0=rows(z[n]), scalar1=0.0, scalar2=None, op0=ALU.max
+                    out=interleaved(z_rounded[n][:]), in0=stacked(sums), scalar1=0.0, scalar2=None, op0=ALU.max
                 )
             else:
-                nc.scalar.activation(out=weave(grouped[:]), in_=rows(z[n]), func=ACT.Relu)
-            rounded[n] = grouped
+                nc.scalar.activation(out=interleaved(z_rounded[n][:]), in_=stacked(sums), func=ACT.Relu)
 
-        def second_product(n, acc):
+        def finish(n, copy):
             width = EDGE_PIECES[n]
+            acc = psum_out.tile([P, width], F32, name="acc_out")
             z_codes = keep.tile([P, width], U32, name=f"z_codes{n}", align_bytes=64)
             z_bytes = keep.tile([P, width], U8, name=f"z_bytes{n}", align_bytes=64)
             nc.vector.quantize_mx(
                 out=z_codes[:].bitcast(FP8X4),
                 scales=z_bytes[:],
-                in_=rounded[n][:].rearrange("p w j -> p (w j)"),
+                in_=z_rounded[n][:].rearrange("p w j -> p (w j)"),
             )
             nc.tensor.matmul_mx(
-                out=acc,
+                out=acc[:],
                 lhsT=w3_codes[:].bitcast(FP8X4),
                 lhsT_scale=w3_bytes[:],
                 rhs=z_codes[:].bitcast(FP8X4),
@@ -203,64 +214,51 @@ def tile_picked_hub_relu_e_kernel(
                 start=True,
                 stop=True,
             )
+            result = keep.tile([P, width], F32, name=f"result{n}")
+            copy(out=result[:], in_=acc[:])
+            nc.sync.dma_start(out=out[:, starts[n] : starts[n] + width], in_=result[:])
 
-        def finish(copy_out, *pieces):
-            width = sum(EDGE_PIECES[n] for n in pieces)
-            a = starts[pieces[0]]
-            acc = psum_out.tile([P, width], F32, name="acc_out")
-            for n in pieces:
-                second_product(n, acc[:, starts[n] - a : starts[n] - a + EDGE_PIECES[n]])
-            result = keep.tile([P, width], F32, name=f"result{pieces[0]}")
-            copy_out(out=result[:], in_=acc[:])
-            nc.sync.dma_start(out=out[:, a : a + width], in_=result[:])
+        sums_half = keep.tile([P, PACK, HALF], F32, name="sums_half", tag="sums_half")
+        sums_third = keep.tile([P, PACK, QUARTER], F32, name="sums_third")
+        sums_last = keep.tile([P, PACK, QUARTER], F32, name="sums_last")
+        third, last = HALF, HALF + QUARTER
+        sources = [keep.tile([P, S if t == 0 else HALF], F32, name=f"sources{t}") for t in range(PACK)]
 
-        Q = 256
-        wide = keep.tile([P, PACK, HALF], F32, name="wide", tag="wide")
-        z[0], z[1] = wide[:, :, :Q], wide[:, :, Q:]
-        for n in range(2, len(EDGE_PIECES)):
-            z[n] = keep.tile([P, PACK, EDGE_PIECES[n]], F32, name=f"z{n}")[:]
-        first = keep.tile([P, S], F32, name="first")
-        turn_a = keep.tile([P, HALF], F32, name="turn_a")
-        turn_b = keep.tile([P, HALF], F32, name="turn_b")
-        turn_c = keep.tile([P, HALF], F32, name="turn_c")
-        low, high = turn_c[:, :Q], turn_c[:, Q:]
+        fetch_source(0, 0, HALF, sources[0][:, :HALF])
+        fetch_source(0, HALF, S, sources[0][:, HALF:])
+        fetch_source(1, 0, HALF, sources[1][:])
+        fetch_source(2, 0, HALF, sources[2][:])
+        add_target(0, 0, HALF, sums_half[:, 0, :], sources[0][:, :HALF])
+        add_target(0, third, last, sums_third[:, 0, :], sources[0][:, third:last])
+        add_target(0, last, S, sums_last[:, 0, :], sources[0][:, last:])
+        add_target(1, 0, HALF, sums_half[:, 1, :], sources[1][:])
+        fetch_source(3, 0, HALF, sources[3][:])
+        add_target(2, 0, HALF, sums_half[:, 2, :], sources[2][:])
+        low, high = sources[3][:, :QUARTER], sources[3][:, QUARTER:]
+        for n, fetched in enumerate((low, high)):
+            cols = slice(n * QUARTER, (n + 1) * QUARTER)
+            add_target(3, cols.start, cols.stop, sums_half[:, 3, cols], fetched)
+            rectify(n, sums_half[:, :, cols])
+            finish(n, nc.scalar.copy)
 
-        fetch_source(0, 0, 512, first[:, :512])
-        fetch_source(0, 512, 1024, first[:, 512:])
-        fetch_source(1, 0, 512, turn_a[:])
-        fetch_source(2, 0, 512, turn_b[:])
-        add_target(0, 0, HALF, wide[:, 0, :], first[:, :HALF])
-        for n in range(2, len(EDGE_PIECES)):
-            a, b = starts[n], starts[n] + EDGE_PIECES[n]
-            add_target(0, a, b, z[n][:, 0, :], first[:, a:b])
-        add_target(1, 0, 512, wide[:, 1, :], turn_a[:])
-        fetch_source(3, 0, 512, turn_c[:])
-        add_target(2, 0, 512, wide[:, 2, :], turn_b[:])
-        add_target(3, 0, Q, z[0][:, 3, :], low)
-        rectify(0)
-        finish(nc.scalar.copy, 0)
-        add_target(3, Q, 512, z[1][:, 3, :], high)
-        rectify(1)
-        finish(nc.scalar.copy, 1)
-        fetch_source(1, 512, 768, low)
-        fetch_source(2, 512, 768, high)
-        add_target(1, 512, 768, z[2][:, 1, :], low)
-        add_target(2, 512, 768, z[2][:, 2, :], high)
-        fetch_source(3, 512, 768, low)
-        fetch_source(1, 768, 1024, high)
-        add_target(3, 512, 768, z[2][:, 3, :], low)
-        rectify(2)
-        add_target(1, 768, 896, z[3][:, 1, :], high[:, :128])
-        fetch_source(2, 768, 1024, low)
-        last = keep.tile([P, Q], F32, name="last", tag="wide")
-        fetch_source(3, 768, 1024, last[:])
-        add_target(2, 768, 896, z[3][:, 2, :], low[:, :128])
-        add_target(3, 768, 896, z[3][:, 3, :], last[:, :128])
-        rectify(3)
-        add_target(1, 896, 1024, z[4][:, 1, :], high[:, 128:])
-        add_target(2, 896, 1024, z[4][:, 2, :], low[:, 128:])
-        add_target(3, 896, 1024, z[4][:, 3, :], last[:, 128:])
-        finish(nc.scalar.copy, 2)
-        rectify(4)
-        finish(nc.scalar.copy, 3)
-        finish(nc.vector.tensor_copy, 4)
+        fetch_source(1, third, last, low)
+        fetch_source(2, third, last, high)
+        add_target(1, third, last, sums_third[:, 1, :], low)
+        add_target(2, third, last, sums_third[:, 2, :], high)
+        fetch_source(3, third, last, low)
+        fetch_source(1, last, S, high)
+        add_target(3, third, last, sums_third[:, 3, :], low)
+        rectify(2, sums_third[:])
+
+        add_target(1, last, S, sums_last[:, 1, :], high)
+        fetch_source(2, last, S, low)
+        spare = keep.tile([P, QUARTER], F32, name="spare", tag="sums_half")
+        fetch_source(3, last, S, spare[:])
+        add_target(2, last, S, sums_last[:, 2, :], low)
+        add_target(3, last, last + EIGHTH, sums_last[:, 3, :EIGHTH], spare[:, :EIGHTH])
+        rectify(3, sums_last[:, :, :EIGHTH])
+        add_target(3, last + EIGHTH, S, sums_last[:, 3, EIGHTH:], spare[:, EIGHTH:])
+        finish(2, nc.scalar.copy)
+        rectify(4, sums_last[:, :, EIGHTH:])
+        finish(3, nc.scalar.copy)
+        finish(4, nc.vector.tensor_copy)

@@ -20,8 +20,9 @@ QUARTER = S // 4
 EIGHTH = S // 8
 FLOPS = 2 * (2 * K * H * S + H * N * S)
 
-X_LOADS = (((1024, 640), (1024, 704)), ((1024, 384), (512, 320), (512, 320)))
 
+SECOND_HALF = ((HALF, HALF + QUARTER), (HALF + QUARTER, S - EIGHTH), (S - EIGHTH, S))
+PLANES = (0, 2, 1, 3)
 EDGE_PIECES = (QUARTER, QUARTER, QUARTER, EIGHTH, EIGHTH)
 
 
@@ -43,7 +44,7 @@ def tile_picked_hub_relu_e_kernel(
     nc = tc.nc
     with ExitStack() as ctx:
         keep = ctx.enter_context(tc.tile_pool(name="keep", bufs=1))
-        psum = ctx.enter_context(tc.psum_pool(name="psum", bufs=5))
+        psum = ctx.enter_context(tc.psum_pool(name="psum", bufs=1))
         psum_out = ctx.enter_context(tc.psum_pool(name="psum_out", bufs=3))
 
         offs_sb = keep.tile([P, S // 16], U16, name="offs_sb")
@@ -55,15 +56,11 @@ def tile_picked_hub_relu_e_kernel(
         nc.vector.memset(w3_bytes[:].bitcast(I32), 0)
 
         x_view = xT.rearrange("(p j) n -> p j n", j=PACK)
-        x_raw = [[], []]
-        for u, loads in enumerate(X_LOADS):
-            c0 = 0
-            for i, (width, cut) in enumerate(loads):
-                raw = keep.tile([P, 2, width], F32, name=f"x_raw{u}{i}")
-                nc.sync.dma_start(out=raw[:], in_=x_view[:, 2 * u : 2 * u + 2, c0 : c0 + width])
-                x_raw[u].append((raw, c0, width, cut))
-                c0 = c0 + width
-            if u == 0:
+        x_raw = {}
+        for j in PLANES:
+            x_raw[j] = keep.tile([P, T], F32, name=f"x_raw{j}")
+            nc.sync.dma_start(out=x_raw[j][:], in_=x_view[:, j, :])
+            if j == 0:
                 nc.sync.dma_start(offs_sb[:], offs)
         w_raw = []
         for i, w in enumerate((w1, w2)):
@@ -82,38 +79,36 @@ def tile_picked_hub_relu_e_kernel(
                 in_=w3_scales[0, 4 * q : 4 * q + 4, :].bitcast(I32),
             )
 
-        pairs = [keep.tile([P, 2 * T], BF16, name=f"pairs{u}") for u in range(2)]
-        gathered = [keep.tile([P, 2, HALF], U32, name=f"gathered{h}") for h in range(2)]
-        for u in range(2):
-            view = pairs[u][:].rearrange("p (c e) -> p c e", e=2)
-            for raw, c0, width, cut in x_raw[u]:
-                nc.scalar.activation(
-                    out=view[:, c0 + cut : c0 + width, :],
-                    in_=raw[:, :, cut:].rearrange("p e c -> p c e"),
-                    func=ACT.Copy,
-                )
-                nc.vector.tensor_copy(out=view[:, c0 : c0 + cut, :], in_=raw[:, :, :cut].rearrange("p e c -> p c e"))
-            second_half = ((1, 0, HALF),) if u == 0 else ((1, 0, QUARTER), (1, QUARTER, HALF))
-            for h, a, b in ((0, 0, HALF),) + second_half:
-                picked_words = pairs[u][:].bitcast(U32).indirect(entries(offs_sb, h * HALF + a, h * HALF + b))
-                nc.vector.tensor_copy(gathered[h][:, u, a:b], picked_words)
+        gathered = [keep.tile([P, 2, QUARTER, 2], BF16, name=f"gathered{q}") for q in range(4)]
+        woven = [keep.tile([P, PACK * QUARTER], BF16, name=f"woven{q}", align_bytes=64) for q in range(4)]
+        for j in PLANES:
+            for q in range(4):
+                offsets = entries(offs_sb, q * QUARTER, (q + 1) * QUARTER)
+                into = gathered[q][:, j // 2, :, j % 2]
+                if j < 2 and q >= 3:
+                    if q == 3:
+                        rounded = keep.tile([P, T], BF16, name=f"x_rounded{j}")
+                        nc.scalar.activation(out=rounded[:], in_=x_raw[j][:], func=ACT.Copy)
+                    nc.scalar.activation(out=into, in_=rounded[:].indirect(offsets), func=ACT.Copy)
+                else:
+                    nc.vector.tensor_copy(into, x_raw[j][:].indirect(offsets))
 
-        woven = [keep.tile([P, PACK * HALF], BF16, name=f"woven{h}", align_bytes=64) for h in range(2)]
-        nc.scalar.copy(
-            out=woven[0][:].bitcast(U32).rearrange("p (c u) -> p c u", u=2),
-            in_=gathered[0][:].rearrange("p u c -> p c u"),
-        )
-        for a in (0, QUARTER):
-            nc.vector.tensor_copy(
-                out=woven[1][:].bitcast(I32).rearrange("p (c u) -> p c u", u=2)[:, a : a + QUARTER, :],
-                in_=gathered[1][:].bitcast(I32).rearrange("p u c -> p c u")[:, a : a + QUARTER, :],
+        def weave(q, copy, dtype):
+            copy(
+                out=woven[q][:].bitcast(dtype).rearrange("p (c u) -> p c u", u=2),
+                in_=gathered[q][:].rearrange("p u c e -> p u (c e)").bitcast(dtype).rearrange("p u c -> p c u"),
             )
+
+        weave(0, nc.scalar.copy, U32)
+        weave(1, nc.scalar.copy, U32)
+        weave(2, nc.vector.tensor_copy, I32)
+        weave(3, nc.vector.tensor_copy, I32)
 
         w_rounded, w_codes, w_bytes = {}, {}, {}
 
-        def round_weight(i, g, copy):
-            w_rounded[i, g] = keep.tile([P, 2, P, PACK], BF16, name=f"w_bf{i}{g}", tag=f"w_bf{i}{g}", align_bytes=64)
-            copy(
+        def round_weight(i, g, tag):
+            w_rounded[i, g] = keep.tile([P, 2, P, PACK], BF16, name=f"w_bf{i}{g}", tag=tag, align_bytes=64)
+            nc.scalar.copy(
                 out=w_rounded[i, g][:].rearrange("p t m j -> p m j t"),
                 in_=w_raw[i][:].rearrange("p j (m t) -> p m j t", t=PACK)[:, :, :, 2 * g : 2 * g + 2],
             )
@@ -127,58 +122,60 @@ def tile_picked_hub_relu_e_kernel(
                 in_=w_rounded[i, g][:].rearrange("p t m j -> p (t m j)"),
             )
 
-        x_codes, x_bytes = {}, {}
+        x_codes = {}
+        x_bytes = keep.tile([P, S], U8, name="x_bytes", align_bytes=64)
 
-        def quantise_picked(h, a, b):
-            nc.vector.quantize_mx(
-                out=x_codes[h][:, a:b].bitcast(FP8X4), scales=x_bytes[h][:, a:b], in_=woven[h][:, PACK * a : PACK * b]
-            )
+        def quantise_picked(a, b, values):
+            h, c = divmod(a, HALF)
+            nc.vector.quantize_mx(out=x_codes[h][:, c : c + b - a].bitcast(FP8X4), scales=x_bytes[:, a:b], in_=values)
 
         x_codes[0] = keep.tile([P, HALF], U32, name="x_codes0", align_bytes=64)
-        x_bytes[0] = keep.tile([P, HALF], U8, name="x_bytes0", align_bytes=64)
-        quantise_picked(0, 0, HALF)
-        round_weight(0, 0, nc.scalar.copy)
+        for q in range(2):
+            quantise_picked(q * QUARTER, (q + 1) * QUARTER, woven[q][:])
+        round_weight(0, 0, "w_bf00")
         quantise_weight(0, 0)
         x_codes[1] = keep.tile([P, HALF], U32, name="x_codes1", tag="w_bf00", align_bytes=64)
-        x_bytes[1] = keep.tile([P, HALF], U8, name="x_bytes1", align_bytes=64)
-        quantise_picked(1, 0, QUARTER)
-        quantise_picked(1, QUARTER, HALF)
-        round_weight(0, 1, nc.scalar.copy)
+        for a, b in SECOND_HALF:
+            q, c = divmod(a, QUARTER)
+            quantise_picked(a, b, woven[q][:, PACK * c : PACK * (c + b - a)])
+        round_weight(0, 1, "w_bf01")
         quantise_weight(0, 1)
-        round_weight(1, 0, nc.vector.tensor_copy)
 
         parts = [[keep.tile([P, S], F32, name=f"part{i}{t}") for t in range(PACK)] for i in range(2)]
 
-        def first_product(i, t, h, a, b, copy):
-            acc = psum.tile([P, b - a], F32, name="acc")
+        def first_product(i, t, a, b, copy, bank):
+            acc = psum.tile([P, b - a], F32, name="acc", tag=f"bank{bank}")
             w_cols = slice((t % 2) * P, (t % 2 + 1) * P)
+            h, c = divmod(a, HALF)
             nc.tensor.matmul_mx(
                 out=acc[:],
                 lhsT=w_codes[i, t // 2][:, w_cols].bitcast(FP8X4),
                 lhsT_scale=w_bytes[i, t // 2][:, w_cols],
-                rhs=x_codes[h][:, a:b].bitcast(FP8X4),
-                rhs_scale=x_bytes[h][:, a:b],
+                rhs=x_codes[h][:, c : c + b - a].bitcast(FP8X4),
+                rhs_scale=x_bytes[:, a:b],
                 start=True,
                 stop=True,
             )
-            copy(out=parts[i][t][:, h * HALF + a : h * HALF + b], in_=acc[:])
+            copy(out=parts[i][t][:, a:b], in_=acc[:])
 
         def whole_tiles(*tiles):
             for i, t in tiles:
                 for h in range(2):
-                    first_product(i, t, h, 0, HALF, nc.scalar.copy)
+                    first_product(i, t, h * HALF, (h + 1) * HALF, nc.scalar.copy, (2 * (PACK * i + t) + h + 3) % 5)
 
-        first_product(0, 0, 0, 0, HALF, nc.scalar.copy)
-        first_product(0, 0, 1, 0, QUARTER, nc.scalar.copy)
-        first_product(0, 0, 1, QUARTER, HALF, nc.vector.tensor_copy)
+        first_product(0, 0, 0, HALF, nc.scalar.copy, 0)
+        for n, (a, b) in enumerate(SECOND_HALF):
+            first_product(0, 0, a, b, nc.scalar.copy if n == len(SECOND_HALF) - 1 else nc.vector.tensor_copy, 2 + n)
+        whole_tiles((0, 1))
+        round_weight(1, 0, "w_bf01")
         quantise_weight(1, 0)
-        whole_tiles((0, 1), (0, 2), (1, 0))
-        round_weight(1, 1, nc.scalar.copy)
+        whole_tiles((0, 2), (0, 3), (1, 0))
+        round_weight(1, 1, "w_bf01")
         quantise_weight(1, 1)
-        whole_tiles((1, 1), (0, 3), (1, 2), (1, 3))
+        whole_tiles((1, 1), (1, 2), (1, 3))
 
         starts = [sum(EDGE_PIECES[:n]) for n in range(len(EDGE_PIECES))]
-        z_rounded = {}
+        z_rounded, acc_out = {}, {}
 
         def fetch_source(t, a, b, into):
             nc.vector.tensor_copy(into, parts[0][t][:].indirect(entries(src_sb, a, b)))
@@ -188,16 +185,11 @@ def tile_picked_hub_relu_e_kernel(
 
         def rectify(n, sums):
             z_rounded[n] = keep.tile([P, EDGE_PIECES[n], PACK], BF16, name=f"z_bf{n}", align_bytes=64)
-            if n == len(EDGE_PIECES) - 1:
-                nc.vector.tensor_scalar(
-                    out=interleaved(z_rounded[n][:]), in0=stacked(sums), scalar1=0.0, scalar2=None, op0=ALU.max
-                )
-            else:
-                nc.scalar.activation(out=interleaved(z_rounded[n][:]), in_=stacked(sums), func=ACT.Relu)
+            nc.scalar.activation(out=interleaved(z_rounded[n][:]), in_=stacked(sums), func=ACT.Relu)
 
-        def finish(n, copy):
+        def second_product(n):
             width = EDGE_PIECES[n]
-            acc = psum_out.tile([P, width], F32, name="acc_out")
+            acc_out[n] = psum_out.tile([P, width], F32, name="acc_out")
             z_codes = keep.tile([P, width], U32, name=f"z_codes{n}", align_bytes=64)
             z_bytes = keep.tile([P, width], U8, name=f"z_bytes{n}", align_bytes=64)
             nc.vector.quantize_mx(
@@ -206,7 +198,7 @@ def tile_picked_hub_relu_e_kernel(
                 in_=z_rounded[n][:].rearrange("p w j -> p (w j)"),
             )
             nc.tensor.matmul_mx(
-                out=acc[:],
+                out=acc_out[n][:],
                 lhsT=w3_codes[:].bitcast(FP8X4),
                 lhsT_scale=w3_bytes[:],
                 rhs=z_codes[:].bitcast(FP8X4),
@@ -214,51 +206,54 @@ def tile_picked_hub_relu_e_kernel(
                 start=True,
                 stop=True,
             )
+
+        def store(n, copy):
+            width = EDGE_PIECES[n]
             result = keep.tile([P, width], F32, name=f"result{n}")
-            copy(out=result[:], in_=acc[:])
+            copy(out=result[:], in_=acc_out[n][:])
             nc.sync.dma_start(out=out[:, starts[n] : starts[n] + width], in_=result[:])
 
-        sums_half = keep.tile([P, PACK, HALF], F32, name="sums_half", tag="sums_half")
-        sums_third = keep.tile([P, PACK, QUARTER], F32, name="sums_third")
-        sums_last = keep.tile([P, PACK, QUARTER], F32, name="sums_last")
+        sums = keep.tile([P, PACK, S], F32, name="sums")
         third, last = HALF, HALF + QUARTER
-        sources = [keep.tile([P, S if t == 0 else HALF], F32, name=f"sources{t}") for t in range(PACK)]
+        sources = [keep.tile([P, S if t < 2 else HALF], F32, name=f"sources{t}") for t in range(PACK)]
 
-        fetch_source(0, 0, HALF, sources[0][:, :HALF])
-        fetch_source(0, HALF, S, sources[0][:, HALF:])
-        fetch_source(1, 0, HALF, sources[1][:])
+        def add_and_place(t, a, b, fetched):
+            add_target(t, a, b, sums[:, t, a:b], fetched)
+
+        def rectify_piece(n):
+            rectify(n, sums[:, :, starts[n] : starts[n] + EDGE_PIECES[n]])
+
+        for t in range(2):
+            fetch_source(t, 0, HALF, sources[t][:, :HALF])
+            fetch_source(t, HALF, S, sources[t][:, HALF:])
         fetch_source(2, 0, HALF, sources[2][:])
-        add_target(0, 0, HALF, sums_half[:, 0, :], sources[0][:, :HALF])
-        add_target(0, third, last, sums_third[:, 0, :], sources[0][:, third:last])
-        add_target(0, last, S, sums_last[:, 0, :], sources[0][:, last:])
-        add_target(1, 0, HALF, sums_half[:, 1, :], sources[1][:])
         fetch_source(3, 0, HALF, sources[3][:])
-        add_target(2, 0, HALF, sums_half[:, 2, :], sources[2][:])
+        for t in range(2):
+            add_and_place(t, 0, HALF, sources[t][:, :HALF])
+            add_and_place(t, HALF, S, sources[t][:, HALF:])
+        add_and_place(2, 0, HALF, sources[2][:])
         low, high = sources[3][:, :QUARTER], sources[3][:, QUARTER:]
         for n, fetched in enumerate((low, high)):
-            cols = slice(n * QUARTER, (n + 1) * QUARTER)
-            add_target(3, cols.start, cols.stop, sums_half[:, 3, cols], fetched)
-            rectify(n, sums_half[:, :, cols])
-            finish(n, nc.scalar.copy)
+            add_and_place(3, n * QUARTER, (n + 1) * QUARTER, fetched)
+            rectify_piece(n)
+        fetch_source(2, third, last, low)
+        fetch_source(3, third, last, high)
+        add_and_place(2, third, last, low)
+        add_and_place(3, third, last, high)
+        rectify_piece(2)
+        second_product(0)
+        second_product(1)
+        store(0, nc.scalar.copy)
+        store(1, nc.scalar.copy)
 
-        fetch_source(1, third, last, low)
-        fetch_source(2, third, last, high)
-        add_target(1, third, last, sums_third[:, 1, :], low)
-        add_target(2, third, last, sums_third[:, 2, :], high)
-        fetch_source(3, third, last, low)
-        fetch_source(1, last, S, high)
-        add_target(3, third, last, sums_third[:, 3, :], low)
-        rectify(2, sums_third[:])
-
-        add_target(1, last, S, sums_last[:, 1, :], high)
-        fetch_source(2, last, S, low)
-        spare = keep.tile([P, QUARTER], F32, name="spare", tag="sums_half")
-        fetch_source(3, last, S, spare[:])
-        add_target(2, last, S, sums_last[:, 2, :], low)
-        add_target(3, last, last + EIGHTH, sums_last[:, 3, :EIGHTH], spare[:, :EIGHTH])
-        rectify(3, sums_last[:, :, :EIGHTH])
-        add_target(3, last + EIGHTH, S, sums_last[:, 3, EIGHTH:], spare[:, EIGHTH:])
-        finish(2, nc.scalar.copy)
-        rectify(4, sums_last[:, :, EIGHTH:])
-        finish(3, nc.scalar.copy)
-        finish(4, nc.vector.tensor_copy)
+        spare = sums[:, 0:2, QUARTER:HALF]
+        for t in (2, 3):
+            fetch_source(t, last, S, spare[:, t - 2, :])
+        for n in range(2):
+            a = n * EIGHTH
+            for t in (2, 3):
+                add_and_place(t, last + a, last + a + EIGHTH, spare[:, t - 2, a : a + EIGHTH])
+            rectify_piece(3 + n)
+        for n in (2, 3, 4):
+            second_product(n)
+            store(n, nc.scalar.copy)

@@ -45,7 +45,6 @@ def tile_picked_hub_relu_e_kernel(
     with ExitStack() as ctx:
         keep = ctx.enter_context(tc.tile_pool(name="keep", bufs=1))
         psum = ctx.enter_context(tc.psum_pool(name="psum", bufs=1))
-        psum_out = ctx.enter_context(tc.psum_pool(name="psum_out", bufs=3))
 
         offs_sb = keep.tile([P, S // 16], U16, name="offs_sb")
         src_sb = keep.tile([P, S // 16], U16, name="src_sb")
@@ -141,7 +140,10 @@ def tile_picked_hub_relu_e_kernel(
         round_weight(0, 1, "w_bf01")
         quantise_weight(0, 1)
 
-        parts = [[keep.tile([P, S], F32, name=f"part{i}{t}") for t in range(PACK)] for i in range(2)]
+        parts = [
+            [x_raw[PLANES[2 * t + i]] if t < 2 else keep.tile([P, S], F32, name=f"part{i}{t}") for t in range(PACK)]
+            for i in range(2)
+        ]
 
         def first_product(i, t, a, b, copy, bank):
             acc = psum.tile([P, b - a], F32, name="acc", tag=f"bank{bank}")
@@ -183,13 +185,17 @@ def tile_picked_hub_relu_e_kernel(
         def add_target(t, a, b, into, fetched):
             nc.vector.tensor_tensor(into, parts[1][t][:].indirect(entries(dst_sb, a, b)), fetched, ALU.add)
 
-        def rectify(n, sums):
-            z_rounded[n] = keep.tile([P, EDGE_PIECES[n], PACK], BF16, name=f"z_bf{n}", align_bytes=64)
-            nc.scalar.activation(out=interleaved(z_rounded[n][:]), in_=stacked(sums), func=ACT.Relu)
+        for n, width in enumerate(EDGE_PIECES):
+            z_rounded[n] = keep.tile([P, width, PACK], BF16, name=f"z_bf{n}", align_bytes=64)
+
+        def rectify(n, sums, t0, t1):
+            nc.scalar.activation(
+                out=interleaved(z_rounded[n][:, :, t0:t1]), in_=stacked(sums[:, t0:t1, :]), func=ACT.Relu
+            )
 
         def second_product(n):
             width = EDGE_PIECES[n]
-            acc_out[n] = psum_out.tile([P, width], F32, name="acc_out")
+            acc_out[n] = psum.tile([P, width], F32, name="acc_out", tag=f"bank{(5 + n) % 8}")
             z_codes = keep.tile([P, width], U32, name=f"z_codes{n}", align_bytes=64)
             z_bytes = keep.tile([P, width], U8, name=f"z_bytes{n}", align_bytes=64)
             nc.vector.quantize_mx(
@@ -220,17 +226,17 @@ def tile_picked_hub_relu_e_kernel(
         def add_and_place(t, a, b, fetched):
             add_target(t, a, b, sums[:, t, a:b], fetched)
 
-        def rectify_piece(n):
-            rectify(n, sums[:, :, starts[n] : starts[n] + EDGE_PIECES[n]])
+        def rectify_piece(n, t0=0, t1=PACK):
+            rectify(n, sums[:, :, starts[n] : starts[n] + EDGE_PIECES[n]], t0, t1)
 
         for t in range(2):
-            fetch_source(t, 0, HALF, sources[t][:, :HALF])
-            fetch_source(t, HALF, S, sources[t][:, HALF:])
+            fetch_source(t, 0, S, sources[t][:])
         fetch_source(2, 0, HALF, sources[2][:])
         fetch_source(3, 0, HALF, sources[3][:])
         for t in range(2):
-            add_and_place(t, 0, HALF, sources[t][:, :HALF])
-            add_and_place(t, HALF, S, sources[t][:, HALF:])
+            add_and_place(t, 0, S, sources[t][:])
+        for n in (3, 4):
+            rectify_piece(n, 0, 2)
         add_and_place(2, 0, HALF, sources[2][:])
         low, high = sources[3][:, :QUARTER], sources[3][:, QUARTER:]
         for n, fetched in enumerate((low, high)):
@@ -242,9 +248,7 @@ def tile_picked_hub_relu_e_kernel(
         add_and_place(3, third, last, high)
         rectify_piece(2)
         second_product(0)
-        second_product(1)
         store(0, nc.scalar.copy)
-        store(1, nc.scalar.copy)
 
         spare = sums[:, 0:2, QUARTER:HALF]
         for t in (2, 3):
@@ -253,7 +257,7 @@ def tile_picked_hub_relu_e_kernel(
             a = n * EIGHTH
             for t in (2, 3):
                 add_and_place(t, last + a, last + a + EIGHTH, spare[:, t - 2, a : a + EIGHTH])
-            rectify_piece(3 + n)
-        for n in (2, 3, 4):
+            rectify_piece(3 + n, 2, PACK)
+        for n in (1, 2, 3, 4):
             second_product(n)
-            store(n, nc.scalar.copy)
+            store(n, nc.vector.tensor_copy if n == 4 else nc.scalar.copy)

@@ -63,8 +63,8 @@ def tile_picked_hub_relu_e_kernel(
                 nc.sync.dma_start(offs_sb[:], offs)
         w_raw = []
         for i, w in enumerate((w1, w2)):
-            raw = keep.tile([P, PACK, H], F32, name=f"w_raw{i}")
-            nc.sync.dma_start(out=raw[:], in_=w.rearrange("(p j) c -> p j c", j=PACK))
+            raw = keep.tile([P, PACK * H], F32, name=f"w_raw{i}")
+            nc.sync.dma_start(out=raw[:], in_=w.rearrange("(p j) c -> p (j c)", j=PACK))
             w_raw.append(raw)
         nc.sync.dma_start(src_sb[:], src)
         nc.sync.dma_start(dst_sb[:], dst)
@@ -109,7 +109,7 @@ def tile_picked_hub_relu_e_kernel(
             w_rounded[i, g] = keep.tile([P, 2, P, PACK], BF16, name=f"w_bf{i}{g}", tag=tag, align_bytes=64)
             nc.scalar.copy(
                 out=w_rounded[i, g][:].rearrange("p t m j -> p m j t"),
-                in_=w_raw[i][:].rearrange("p j (m t) -> p m j t", t=PACK)[:, :, :, 2 * g : 2 * g + 2],
+                in_=w_raw[i][:].rearrange("p (j m t) -> p m j t", j=PACK, t=PACK)[:, :, :, 2 * g : 2 * g + 2],
             )
 
         def quantise_weight(i, g):
@@ -141,8 +141,8 @@ def tile_picked_hub_relu_e_kernel(
         quantise_weight(0, 1)
 
         parts = [
-            [x_raw[PLANES[2 * t + i]] if t < 2 else keep.tile([P, S], F32, name=f"part{i}{t}") for t in range(PACK)]
-            for i in range(2)
+            [x_raw[j] for j in PLANES],
+            w_raw + [keep.tile([P, S], F32, name=f"part1{t}") for t in (2, 3)],
         ]
 
         def first_product(i, t, a, b, copy, bank):
@@ -160,21 +160,35 @@ def tile_picked_hub_relu_e_kernel(
             )
             copy(out=parts[i][t][:, a:b], in_=acc[:])
 
-        def whole_tiles(*tiles):
-            for i, t in tiles:
-                for h in range(2):
-                    first_product(i, t, h * HALF, (h + 1) * HALF, nc.scalar.copy, (2 * (PACK * i + t) + h + 3) % 5)
-
         first_product(0, 0, 0, HALF, nc.scalar.copy, 0)
         for n, (a, b) in enumerate(SECOND_HALF):
             first_product(0, 0, a, b, nc.scalar.copy if n == len(SECOND_HALF) - 1 else nc.vector.tensor_copy, 2 + n)
-        whole_tiles((0, 1))
+        turn = [0]
+
+        def products(i, t, *ranges):
+            for a, b in ranges or ((0, HALF), (HALF, S)):
+                first_product(i, t, a, b, nc.scalar.copy, turn[0] % 5)
+                turn[0] = turn[0] + 1
+
+        products(0, 1)
         round_weight(1, 0, "w_bf01")
         quantise_weight(1, 0)
-        whole_tiles((0, 2), (0, 3), (1, 0))
+        products(0, 2)
         round_weight(1, 1, "w_bf01")
         quantise_weight(1, 1)
-        whole_tiles((1, 1), (1, 2), (1, 3))
+        products(1, 0)
+        products(1, 1)
+        products(0, 3)
+        products(1, 2, (0, HALF))
+        products(1, 3, (0, HALF), (HALF, HALF + QUARTER))
+        products(1, 2, (HALF, S))
+        products(1, 3, (HALF + QUARTER, S))
+
+        last = HALF + QUARTER
+
+        def clock(view):
+            tick = keep.tile([P, 1], F32, name="tick", bufs=4)
+            nc.gpsimd.tensor_copy(tick[:], view)
 
         starts = [sum(EDGE_PIECES[:n]) for n in range(len(EDGE_PIECES))]
         z_rounded, acc_out = {}, {}
@@ -187,11 +201,6 @@ def tile_picked_hub_relu_e_kernel(
 
         for n, width in enumerate(EDGE_PIECES):
             z_rounded[n] = keep.tile([P, width, PACK], BF16, name=f"z_bf{n}", align_bytes=64)
-
-        def rectify(n, sums, t0, t1):
-            nc.scalar.activation(
-                out=interleaved(z_rounded[n][:, :, t0:t1]), in_=stacked(sums[:, t0:t1, :]), func=ACT.Relu
-            )
 
         def second_product(n):
             width = EDGE_PIECES[n]
@@ -219,45 +228,39 @@ def tile_picked_hub_relu_e_kernel(
             copy(out=result[:], in_=acc_out[n][:])
             nc.sync.dma_start(out=out[:, starts[n] : starts[n] + width], in_=result[:])
 
-        sums = keep.tile([P, PACK, S], F32, name="sums")
-        third, last = HALF, HALF + QUARTER
-        sources = [keep.tile([P, S if t < 2 else HALF], F32, name=f"sources{t}") for t in range(PACK)]
+        early = keep.tile([P, 2, S], F32, name="early")
+        late = keep.tile([P, 2 * last], F32, name="late")
+        first = late[:, QUARTER : QUARTER + S].rearrange("p (t c) -> p t c", t=2)
+        second = late[:].rearrange("p (t c) -> p t c", t=2)
+        sources = [keep.tile([P, S if t < 3 else HALF], F32, name=f"sources{t}") for t in range(PACK)]
 
-        def add_and_place(t, a, b, fetched):
-            add_target(t, a, b, sums[:, t, a:b], fetched)
+        def add_into(sums, t, a, b):
+            reused = t == 3 and a >= HALF
+            add_target(t, a, b, sums, sources[2][:, a - HALF : b - HALF] if reused else sources[t][:, a:b])
 
-        def rectify_piece(n, t0=0, t1=PACK):
-            rectify(n, sums[:, :, starts[n] : starts[n] + EDGE_PIECES[n]], t0, t1)
+        def rectify(n, t, pair):
+            nc.scalar.activation(out=interleaved(z_rounded[n][:, :, t : t + 2]), in_=stacked(pair), func=ACT.Relu)
 
-        for t in range(2):
+        for t in range(3):
             fetch_source(t, 0, S, sources[t][:])
-        fetch_source(2, 0, HALF, sources[2][:])
-        fetch_source(3, 0, HALF, sources[3][:])
         for t in range(2):
-            add_and_place(t, 0, S, sources[t][:])
-        for n in (3, 4):
-            rectify_piece(n, 0, 2)
-        add_and_place(2, 0, HALF, sources[2][:])
-        low, high = sources[3][:, :QUARTER], sources[3][:, QUARTER:]
-        for n, fetched in enumerate((low, high)):
-            add_and_place(3, n * QUARTER, (n + 1) * QUARTER, fetched)
-            rectify_piece(n)
-        fetch_source(2, third, last, low)
-        fetch_source(3, third, last, high)
-        add_and_place(2, third, last, low)
-        add_and_place(3, third, last, high)
-        rectify_piece(2)
+            add_into(early[:, t, :], t, 0, S)
+        fetch_source(3, 0, HALF, sources[3][:])
+        for n, width in enumerate(EDGE_PIECES):
+            rectify(n, 0, early[:, :, starts[n] : starts[n] + width])
+        add_into(first[:, 0, :], 2, 0, HALF)
+        add_into(first[:, 1, :], 3, 0, HALF)
+        for n in range(2):
+            rectify(n, 2, first[:, :, starts[n] : starts[n] + QUARTER])
         second_product(0)
         store(0, nc.scalar.copy)
-
-        spare = sums[:, 0:2, QUARTER:HALF]
-        for t in (2, 3):
-            fetch_source(t, last, S, spare[:, t - 2, :])
-        for n in range(2):
-            a = n * EIGHTH
-            for t in (2, 3):
-                add_and_place(t, last + a, last + a + EIGHTH, spare[:, t - 2, a : a + EIGHTH])
-            rectify_piece(3 + n, 2, PACK)
+        fetch_source(3, HALF, S, sources[2][:, :HALF])
+        for a in (0, QUARTER):
+            add_into(second[:, 0, a : a + QUARTER], 2, HALF + a, last + a)
+            for n in (3, 4) if a else (2,):
+                cols = slice(starts[n] - HALF, starts[n] - HALF + EDGE_PIECES[n])
+                add_into(second[:, 1, cols], 3, starts[n], starts[n] + EDGE_PIECES[n])
+                rectify(n, 2, second[:, :, cols])
         for n in (1, 2, 3, 4):
             second_product(n)
             store(n, nc.vector.tensor_copy if n == 4 else nc.scalar.copy)

@@ -21,9 +21,7 @@ EIGHTH = S // 8
 FLOPS = 2 * (2 * K * H * S + H * N * S)
 
 
-SECOND_HALF = ((HALF, HALF + QUARTER), (HALF + QUARTER, S - EIGHTH), (S - EIGHTH, S))
-PLANES = (0, 2, 1, 3)
-EDGE_PIECES = (QUARTER, QUARTER, QUARTER, EIGHTH, EIGHTH)
+END_PIECES = ((0, QUARTER), (QUARTER, HALF), (HALF, HALF + QUARTER), (HALF + QUARTER, S - EIGHTH), (S - EIGHTH, S))
 
 
 def interleaved(view):
@@ -55,9 +53,9 @@ def tile_picked_hub_relu_e_kernel(
         nc.vector.memset(w3_bytes[:].bitcast(I32), 0)
 
         x_view = xT.rearrange("(p j) n -> p j n", j=PACK)
-        x_raw = {}
-        for j in PLANES:
-            x_raw[j] = keep.tile([P, T], F32, name=f"x_raw{j}")
+        x_raw = []
+        for j in range(PACK):
+            x_raw.append(keep.tile([P, T], F32, name=f"x_raw{j}"))
             nc.sync.dma_start(out=x_raw[j][:], in_=x_view[:, j, :])
             if j == 0:
                 nc.sync.dma_start(offs_sb[:], offs)
@@ -78,36 +76,38 @@ def tile_picked_hub_relu_e_kernel(
                 in_=w3_scales[0, 4 * q : 4 * q + 4, :].bitcast(I32),
             )
 
-        gathered = [keep.tile([P, 2, QUARTER, 2], BF16, name=f"gathered{q}") for q in range(4)]
-        woven = [keep.tile([P, PACK * QUARTER], BF16, name=f"woven{q}", align_bytes=64) for q in range(4)]
-        for j in PLANES:
-            for q in range(4):
-                offsets = entries(offs_sb, q * QUARTER, (q + 1) * QUARTER)
-                into = gathered[q][:, j // 2, :, j % 2]
-                if j < 2 and q >= 3:
-                    if q == 3:
-                        rounded = keep.tile([P, T], BF16, name=f"x_rounded{j}")
-                        nc.scalar.activation(out=rounded[:], in_=x_raw[j][:], func=ACT.Copy)
-                    nc.scalar.activation(out=into, in_=rounded[:].indirect(offsets), func=ACT.Copy)
-                else:
-                    nc.vector.tensor_copy(into, x_raw[j][:].indirect(offsets))
+        def on_scalar(into, window, offsets):
+            nc.scalar.activation(out=into, in_=window[:].indirect(offsets), func=ACT.Copy)
 
-        def weave(q, copy, dtype):
-            copy(
-                out=woven[q][:].bitcast(dtype).rearrange("p (c u) -> p c u", u=2),
-                in_=gathered[q][:].rearrange("p u c e -> p u (c e)").bitcast(dtype).rearrange("p u c -> p c u"),
+        def on_vector(into, window, offsets):
+            nc.vector.tensor_copy(into, window[:].indirect(offsets))
+
+        woven = [keep.tile([P, QUARTER, PACK], BF16, name=f"woven{q}", align_bytes=64) for q in range(4)]
+        x_codes = keep.tile([P, S], U32, name="x_codes", align_bytes=64)
+        x_bytes = keep.tile([P, S], U8, name="x_bytes", align_bytes=64)
+
+        def quantise_picked(q):
+            cols = slice(q * QUARTER, (q + 1) * QUARTER)
+            nc.vector.quantize_mx(
+                out=x_codes[:, cols].bitcast(FP8X4),
+                scales=x_bytes[:, cols],
+                in_=woven[q][:].rearrange("p c j -> p (c j)"),
             )
 
-        weave(0, nc.scalar.copy, U32)
-        weave(1, nc.scalar.copy, U32)
-        weave(2, nc.vector.tensor_copy, I32)
-        weave(3, nc.vector.tensor_copy, I32)
+        for j in range(PACK):
+            for q in range(4):
+                picked = keep.tile([P, QUARTER], BF16, name=f"picked{j}{q}")
+                on_scalar(picked[:], x_raw[j], entries(offs_sb, q * QUARTER, (q + 1) * QUARTER))
+                nc.vector.tensor_copy(woven[q][:, :, j], picked[:])
+                if j == PACK - 1 and q > 0:
+                    quantise_picked(q - 1)
+        quantise_picked(3)
 
         w_rounded, w_codes, w_bytes = {}, {}, {}
 
-        def round_weight(i, g, tag):
-            w_rounded[i, g] = keep.tile([P, 2, P, PACK], BF16, name=f"w_bf{i}{g}", tag=tag, align_bytes=64)
-            nc.scalar.copy(
+        def round_weight(i, g, copy):
+            w_rounded[i, g] = keep.tile([P, 2, P, PACK], BF16, name=f"w_bf{i}{g}", align_bytes=64)
+            copy(
                 out=w_rounded[i, g][:].rearrange("p t m j -> p m j t"),
                 in_=w_raw[i][:].rearrange("p (j m t) -> p m j t", j=PACK, t=PACK)[:, :, :, 2 * g : 2 * g + 2],
             )
@@ -121,92 +121,62 @@ def tile_picked_hub_relu_e_kernel(
                 in_=w_rounded[i, g][:].rearrange("p t m j -> p (t m j)"),
             )
 
-        x_codes = {}
-        x_bytes = keep.tile([P, S], U8, name="x_bytes", align_bytes=64)
+        parts = [[keep.tile([P, S], F32, name=f"part{i}{t}") for t in range(PACK)] for i in range(2)]
+        turn = [0]
 
-        def quantise_picked(a, b, values):
-            h, c = divmod(a, HALF)
-            nc.vector.quantize_mx(out=x_codes[h][:, c : c + b - a].bitcast(FP8X4), scales=x_bytes[:, a:b], in_=values)
-
-        x_codes[0] = keep.tile([P, HALF], U32, name="x_codes0", align_bytes=64)
-        for q in range(2):
-            quantise_picked(q * QUARTER, (q + 1) * QUARTER, woven[q][:])
-        round_weight(0, 0, "w_bf00")
-        quantise_weight(0, 0)
-        x_codes[1] = keep.tile([P, HALF], U32, name="x_codes1", tag="w_bf00", align_bytes=64)
-        for a, b in SECOND_HALF:
-            q, c = divmod(a, QUARTER)
-            quantise_picked(a, b, woven[q][:, PACK * c : PACK * (c + b - a)])
-        round_weight(0, 1, "w_bf01")
-        quantise_weight(0, 1)
-
-        parts = [
-            [x_raw[j] for j in PLANES],
-            w_raw + [keep.tile([P, S], F32, name=f"part1{t}") for t in (2, 3)],
-        ]
-
-        def first_product(i, t, a, b, copy, bank):
-            acc = psum.tile([P, b - a], F32, name="acc", tag=f"bank{bank}")
+        def first_product(i, t, a, b, copy):
+            acc = psum.tile([P, b - a], F32, name="acc", tag=f"bank{turn[0] % 5}")
+            turn[0] = turn[0] + 1
             w_cols = slice((t % 2) * P, (t % 2 + 1) * P)
-            h, c = divmod(a, HALF)
             nc.tensor.matmul_mx(
                 out=acc[:],
                 lhsT=w_codes[i, t // 2][:, w_cols].bitcast(FP8X4),
                 lhsT_scale=w_bytes[i, t // 2][:, w_cols],
-                rhs=x_codes[h][:, c : c + b - a].bitcast(FP8X4),
+                rhs=x_codes[:, a:b].bitcast(FP8X4),
                 rhs_scale=x_bytes[:, a:b],
                 start=True,
                 stop=True,
             )
             copy(out=parts[i][t][:, a:b], in_=acc[:])
 
-        first_product(0, 0, 0, HALF, nc.scalar.copy, 0)
-        for n, (a, b) in enumerate(SECOND_HALF):
-            first_product(0, 0, a, b, nc.scalar.copy if n == len(SECOND_HALF) - 1 else nc.vector.tensor_copy, 2 + n)
-        turn = [0]
+        def products(i, t, first, second):
+            first_product(i, t, 0, HALF, first)
+            first_product(i, t, HALF, S, second)
 
-        def products(i, t, *ranges):
-            for a, b in ranges or ((0, HALF), (HALF, S)):
-                first_product(i, t, a, b, nc.scalar.copy, turn[0] % 5)
-                turn[0] = turn[0] + 1
+        scalar, vector = nc.scalar.copy, nc.vector.tensor_copy
+        sources = {}
+        sums = [keep.tile([P, PACK, HALF], F32, name=f"sums{h}") for h in range(2)]
 
-        products(0, 1)
-        round_weight(1, 0, "w_bf01")
-        quantise_weight(1, 0)
-        products(0, 2)
-        round_weight(1, 1, "w_bf01")
-        quantise_weight(1, 1)
-        products(1, 0)
-        products(1, 1)
-        products(0, 3)
-        products(1, 2, (0, HALF))
-        products(1, 3, (0, HALF), (HALF, HALF + QUARTER))
-        products(1, 2, (HALF, S))
-        products(1, 3, (HALF + QUARTER, S))
+        def fetch_source(t, h, gather):
+            sources[t, h] = keep.tile([P, HALF], F32, name=f"sources{t}{h}")
+            gather(sources[t, h][:], parts[0][t], entries(src_sb, h * HALF, (h + 1) * HALF))
 
-        last = HALF + QUARTER
+        def add_target(t, a, b):
+            h, c = divmod(a, HALF)
+            nc.vector.tensor_tensor(
+                sums[h][:, t, c : c + b - a],
+                parts[1][t][:].indirect(entries(dst_sb, a, b)),
+                sources[t, h][:, c : c + b - a],
+                ALU.add,
+            )
 
-        def clock(view):
-            tick = keep.tile([P, 1], F32, name="tick", bufs=4)
-            nc.gpsimd.tensor_copy(tick[:], view)
-
-        starts = [sum(EDGE_PIECES[:n]) for n in range(len(EDGE_PIECES))]
         z_rounded, acc_out = {}, {}
 
-        def fetch_source(t, a, b, into):
-            nc.vector.tensor_copy(into, parts[0][t][:].indirect(entries(src_sb, a, b)))
-
-        def add_target(t, a, b, into, fetched):
-            nc.vector.tensor_tensor(into, parts[1][t][:].indirect(entries(dst_sb, a, b)), fetched, ALU.add)
-
-        for n, width in enumerate(EDGE_PIECES):
-            z_rounded[n] = keep.tile([P, width, PACK], BF16, name=f"z_bf{n}", align_bytes=64)
+        def rectify(n, on_act):
+            a, b = END_PIECES[n]
+            h, c = divmod(a, HALF)
+            z_rounded[n] = keep.tile([P, b - a, PACK], BF16, name=f"z_bf{n}", align_bytes=64)
+            into, values = interleaved(z_rounded[n][:]), stacked(sums[h][:, :, c : c + b - a])
+            if on_act:
+                nc.scalar.activation(out=into, in_=values, func=ACT.Relu)
+            else:
+                nc.vector.tensor_scalar_max(into, values, 0.0)
 
         def second_product(n):
-            width = EDGE_PIECES[n]
-            acc_out[n] = psum.tile([P, width], F32, name="acc_out", tag=f"bank{(5 + n) % 8}")
-            z_codes = keep.tile([P, width], U32, name=f"z_codes{n}", align_bytes=64)
-            z_bytes = keep.tile([P, width], U8, name=f"z_bytes{n}", align_bytes=64)
+            a, b = END_PIECES[n]
+            acc_out[n] = psum.tile([P, b - a], F32, name="acc_out", tag=f"bank{(5 + n) % 8}")
+            z_codes = keep.tile([P, b - a], U32, name=f"z_codes{n}", align_bytes=64)
+            z_bytes = keep.tile([P, b - a], U8, name=f"z_bytes{n}", align_bytes=64)
             nc.vector.quantize_mx(
                 out=z_codes[:].bitcast(FP8X4),
                 scales=z_bytes[:],
@@ -223,44 +193,57 @@ def tile_picked_hub_relu_e_kernel(
             )
 
         def store(n, copy):
-            width = EDGE_PIECES[n]
-            result = keep.tile([P, width], F32, name=f"result{n}")
+            a, b = END_PIECES[n]
+            result = keep.tile([P, b - a], F32, name=f"result{n}")
             copy(out=result[:], in_=acc_out[n][:])
-            nc.sync.dma_start(out=out[:, starts[n] : starts[n] + width], in_=result[:])
+            nc.sync.dma_start(out=out[:, a:b], in_=result[:])
 
-        early = keep.tile([P, 2, S], F32, name="early")
-        late = keep.tile([P, 2 * last], F32, name="late")
-        first = late[:, QUARTER : QUARTER + S].rearrange("p (t c) -> p t c", t=2)
-        second = late[:].rearrange("p (t c) -> p t c", t=2)
-        sources = [keep.tile([P, S if t < 3 else HALF], F32, name=f"sources{t}") for t in range(PACK)]
-
-        def add_into(sums, t, a, b):
-            reused = t == 3 and a >= HALF
-            add_target(t, a, b, sums, sources[2][:, a - HALF : b - HALF] if reused else sources[t][:, a:b])
-
-        def rectify(n, t, pair):
-            nc.scalar.activation(out=interleaved(z_rounded[n][:, :, t : t + 2]), in_=stacked(pair), func=ACT.Relu)
-
-        for t in range(3):
-            fetch_source(t, 0, S, sources[t][:])
-        for t in range(2):
-            add_into(early[:, t, :], t, 0, S)
-        fetch_source(3, 0, HALF, sources[3][:])
-        for n, width in enumerate(EDGE_PIECES):
-            rectify(n, 0, early[:, :, starts[n] : starts[n] + width])
-        add_into(first[:, 0, :], 2, 0, HALF)
-        add_into(first[:, 1, :], 3, 0, HALF)
-        for n in range(2):
-            rectify(n, 2, first[:, :, starts[n] : starts[n] + QUARTER])
+        round_weight(0, 0, scalar)
+        quantise_weight(0, 0)
+        round_weight(0, 1, vector)
+        for q in range(4):
+            first_product(0, 0, q * QUARTER, (q + 1) * QUARTER, vector if q == 2 else scalar)
+        fetch_source(0, 0, on_scalar)
+        round_weight(1, 0, vector)
+        quantise_weight(0, 1)
+        products(0, 1, vector, scalar)
+        quantise_weight(1, 0)
+        fetch_source(1, 0, on_scalar)
+        round_weight(1, 1, vector)
+        products(1, 0, vector, vector)
+        quantise_weight(1, 1)
+        add_target(0, 0, HALF)
+        products(0, 2, scalar, scalar)
+        products(1, 1, scalar, scalar)
+        products(1, 3, vector, vector)
+        fetch_source(2, 0, on_scalar)
+        add_target(1, 0, HALF)
+        products(1, 2, scalar, scalar)
+        fetch_source(0, 1, on_vector)
+        products(0, 3, scalar, scalar)
+        add_target(2, 0, HALF)
+        fetch_source(3, 0, on_scalar)
+        add_target(0, HALF, S)
+        fetch_source(1, 1, on_scalar)
+        add_target(3, 0, HALF)
+        fetch_source(2, 1, on_scalar)
+        add_target(1, HALF, S)
+        fetch_source(3, 1, on_scalar)
+        add_target(2, HALF, S)
+        rectify(0, True)
+        rectify(1, True)
+        for n in (2, 3, 4):
+            add_target(3, *END_PIECES[n])
         second_product(0)
-        store(0, nc.scalar.copy)
-        fetch_source(3, HALF, S, sources[2][:, :HALF])
-        for a in (0, QUARTER):
-            add_into(second[:, 0, a : a + QUARTER], 2, HALF + a, last + a)
-            for n in (3, 4) if a else (2,):
-                cols = slice(starts[n] - HALF, starts[n] - HALF + EDGE_PIECES[n])
-                add_into(second[:, 1, cols], 3, starts[n], starts[n] + EDGE_PIECES[n])
-                rectify(n, 2, second[:, :, cols])
-        for n in (1, 2, 3, 4):
-            second_product(n)
-            store(n, nc.vector.tensor_copy if n == 4 else nc.scalar.copy)
+        store(0, scalar)
+        rectify(2, False)
+        second_product(1)
+        store(1, scalar)
+        rectify(3, False)
+        second_product(2)
+        store(2, scalar)
+        rectify(4, False)
+        second_product(3)
+        store(3, scalar)
+        second_product(4)
+        store(4, vector)

@@ -21,7 +21,7 @@ EIGHTH = S // 8
 FLOPS = 2 * (2 * K * H * S + H * N * S)
 
 
-END_PIECES = ((0, QUARTER), (QUARTER, HALF), (HALF, HALF + QUARTER), (HALF + QUARTER, S - EIGHTH), (S - EIGHTH, S))
+END_PIECES = ((0, 2), (2, 3), (3, 4), (5, 7), (4, 5), (7, 8))
 
 
 def interleaved(view):
@@ -60,7 +60,7 @@ def tile_picked_hub_relu_e_kernel(
             if j == 0:
                 nc.sync.dma_start(offs_sb[:], offs)
         w_raw = []
-        for i, w in enumerate((w1, w2)):
+        for i, w in enumerate((w2, w1)):
             raw = keep.tile([P, PACK * H], F32, name=f"w_raw{i}")
             nc.sync.dma_start(out=raw[:], in_=w.rearrange("(p j) c -> p (j c)", j=PACK))
             w_raw.append(raw)
@@ -77,104 +77,118 @@ def tile_picked_hub_relu_e_kernel(
             )
 
         def on_scalar(into, window, offsets):
-            nc.scalar.activation(out=into, in_=window[:].indirect(offsets), func=ACT.Copy)
+            nc.scalar.activation(out=into, in_=window.indirect(offsets), func=ACT.Copy)
 
         def on_vector(into, window, offsets):
-            nc.vector.tensor_copy(into, window[:].indirect(offsets))
+            nc.vector.tensor_copy(into, window.indirect(offsets))
 
         woven = [keep.tile([P, QUARTER, PACK], BF16, name=f"woven{q}", align_bytes=64) for q in range(4)]
-        x_codes = keep.tile([P, S], U32, name="x_codes", align_bytes=64)
+        x_codes = {0: keep.tile([P, HALF], U32, name="x_codes0", align_bytes=64)}
         x_bytes = keep.tile([P, S], U8, name="x_bytes", align_bytes=64)
 
         def quantise_picked(q):
             cols = slice(q * QUARTER, (q + 1) * QUARTER)
             nc.vector.quantize_mx(
-                out=x_codes[:, cols].bitcast(FP8X4),
+                out=x_codes[q // 2][:, (q % 2) * QUARTER : (q % 2 + 1) * QUARTER].bitcast(FP8X4),
                 scales=x_bytes[:, cols],
                 in_=woven[q][:].rearrange("p c j -> p (c j)"),
             )
 
-        for j in range(PACK):
+        picked = [keep.tile([P, PACK, QUARTER], BF16, name=f"picked{q}") for q in range(4)]
+
+        def look_up(j, q, gather, into):
+            gather(into, x_raw[j][:], entries(offs_sb, q * QUARTER, (q + 1) * QUARTER))
+
+        for j in range(PACK - 1):
             for q in range(4):
-                picked = keep.tile([P, QUARTER], BF16, name=f"picked{j}{q}")
-                on_scalar(picked[:], x_raw[j], entries(offs_sb, q * QUARTER, (q + 1) * QUARTER))
-                nc.vector.tensor_copy(woven[q][:, :, j], picked[:])
-                if j == PACK - 1 and q > 0:
-                    quantise_picked(q - 1)
-        quantise_picked(3)
+                look_up(j, q, on_vector if q < PACK - 1 - j else on_scalar, picked[q][:, j, :])
+        def weave(q, planes, copy):
+            copy(interleaved(woven[q][:, :, :planes]), stacked(picked[q][:, :planes, :]))
+
+        for q in range(3):
+            weave(q, PACK - 1, nc.vector.tensor_copy)
+        look_up(PACK - 1, 0, on_vector, woven[0][:, :, PACK - 1])
+        for q in range(1, 4):
+            look_up(PACK - 1, q, on_scalar, picked[q][:, PACK - 1, :])
+            if q < 3:
+                nc.vector.tensor_copy(woven[q][:, :, PACK - 1], picked[q][:, PACK - 1, :])
+        quantise_picked(0)
+        weave(3, PACK, nc.scalar.copy)
 
         w_rounded, w_codes, w_bytes = {}, {}, {}
 
-        def round_weight(i, g, copy):
-            w_rounded[i, g] = keep.tile([P, 2, P, PACK], BF16, name=f"w_bf{i}{g}", align_bytes=64)
+        def round_weight(i, g, copy, tag):
+            w_rounded[i, g] = keep.tile([P, 2, P, PACK], BF16, name=f"w_bf{i}{g}", tag=tag, align_bytes=64)
             copy(
                 out=w_rounded[i, g][:].rearrange("p t m j -> p m j t"),
                 in_=w_raw[i][:].rearrange("p (j m t) -> p m j t", j=PACK, t=PACK)[:, :, :, 2 * g : 2 * g + 2],
             )
 
-        def quantise_weight(i, g):
-            w_codes[i, g] = keep.tile([P, 2 * P], U32, name=f"w_codes{i}{g}", align_bytes=64)
-            w_bytes[i, g] = keep.tile([P, 2 * P], U8, name=f"w_bytes{i}{g}", align_bytes=64)
+        def quantise_weight(i, tiles, tag):
+            codes = keep.tile([P, len(tiles) * P], U32, name=f"w_codes{i}{tiles[0]}", tag=tag, align_bytes=64)
+            scales = keep.tile([P, len(tiles) * P], U8, name=f"w_bytes{i}{tiles[0]}", align_bytes=64)
+            g, first = divmod(tiles[0], 2)
             nc.vector.quantize_mx(
-                out=w_codes[i, g][:].bitcast(FP8X4),
-                scales=w_bytes[i, g][:],
-                in_=w_rounded[i, g][:].rearrange("p t m j -> p (t m j)"),
+                out=codes[:].bitcast(FP8X4),
+                scales=scales[:],
+                in_=w_rounded[i, g][:, first : first + len(tiles)].rearrange("p t m j -> p (t m j)"),
             )
+            for n, t in enumerate(tiles):
+                w_codes[i, t] = codes[:, n * P : (n + 1) * P]
+                w_bytes[i, t] = scales[:, n * P : (n + 1) * P]
 
-        parts = [[keep.tile([P, S], F32, name=f"part{i}{t}") for t in range(PACK)] for i in range(2)]
-        turn = [0]
+        targets = keep.tile([P, (PACK - 1) * S], F32, name="targets")
+        parts = [
+            [x_raw[0][:]] + [targets[:, t * S : (t + 1) * S] for t in range(PACK - 1)],
+            [x_raw[1][:]] + [keep.tile([P, S], F32, name=f"sources{t}")[:] for t in range(1, PACK)],
+        ]
 
-        def first_product(i, t, a, b, copy):
-            acc = psum.tile([P, b - a], F32, name="acc", tag=f"bank{turn[0] % 5}")
-            turn[0] = turn[0] + 1
-            w_cols = slice((t % 2) * P, (t % 2 + 1) * P)
+        def first_product(i, t, a, b, copy, bank):
+            acc = psum.tile([P, b - a], F32, name="acc", tag=f"bank{bank}")
             nc.tensor.matmul_mx(
                 out=acc[:],
-                lhsT=w_codes[i, t // 2][:, w_cols].bitcast(FP8X4),
-                lhsT_scale=w_bytes[i, t // 2][:, w_cols],
-                rhs=x_codes[:, a:b].bitcast(FP8X4),
+                lhsT=w_codes[i, t].bitcast(FP8X4),
+                lhsT_scale=w_bytes[i, t],
+                rhs=x_codes[a // HALF][:, a % HALF : a % HALF + b - a].bitcast(FP8X4),
                 rhs_scale=x_bytes[:, a:b],
                 start=True,
                 stop=True,
             )
             copy(out=parts[i][t][:, a:b], in_=acc[:])
 
-        def products(i, t, first, second):
-            first_product(i, t, 0, HALF, first)
-            first_product(i, t, HALF, S, second)
+        def products(i, t, first, second, banks):
+            first_product(i, t, 0, HALF, first, banks[0])
+            first_product(i, t, HALF, S, second, banks[1])
 
         scalar, vector = nc.scalar.copy, nc.vector.tensor_copy
-        sources = {}
-        sums = [keep.tile([P, PACK, HALF], F32, name=f"sums{h}") for h in range(2)]
+        fetched = keep.tile([P, PACK, S], F32, name="fetched")
+        sums = keep.tile([P, PACK, S], F32, name="sums")
 
-        def fetch_source(t, h, gather):
-            sources[t, h] = keep.tile([P, HALF], F32, name=f"sources{t}{h}")
-            gather(sources[t, h][:], parts[0][t], entries(src_sb, h * HALF, (h + 1) * HALF))
+        def fetch_target(t, a, b, upto):
+            window = targets[:, (t - 1) * S : upto * S] if t else parts[0][0]
+            on_scalar(fetched[:, t, a:b], window, entries(dst_sb, a, b))
 
-        def add_target(t, a, b):
-            h, c = divmod(a, HALF)
+        def add_source(t, a, b):
             nc.vector.tensor_tensor(
-                sums[h][:, t, c : c + b - a],
-                parts[1][t][:].indirect(entries(dst_sb, a, b)),
-                sources[t, h][:, c : c + b - a],
-                ALU.add,
+                sums[:, t, a:b], parts[1][t].indirect(entries(src_sb, a, b)), fetched[:, t, a:b], ALU.add
             )
 
         z_rounded, acc_out = {}, {}
 
-        def rectify(n, on_act):
-            a, b = END_PIECES[n]
-            h, c = divmod(a, HALF)
+        def rectify(n, share):
+            a, b = (EIGHTH * e for e in END_PIECES[n])
             z_rounded[n] = keep.tile([P, b - a, PACK], BF16, name=f"z_bf{n}", align_bytes=64)
-            into, values = interleaved(z_rounded[n][:]), stacked(sums[h][:, :, c : c + b - a])
-            if on_act:
-                nc.scalar.activation(out=into, in_=values, func=ACT.Relu)
-            else:
-                nc.vector.tensor_scalar_max(into, values, 0.0)
+            if share:
+                nc.scalar.activation(
+                    out=interleaved(z_rounded[n][:, :share]), in_=stacked(sums[:, :, a : a + share]), func=ACT.Relu
+                )
+            if share < b - a:
+                nc.vector.tensor_scalar_max(
+                    interleaved(z_rounded[n][:, share:]), stacked(sums[:, :, a + share : b]), 0.0
+                )
 
-        def second_product(n):
-            a, b = END_PIECES[n]
-            acc_out[n] = psum.tile([P, b - a], F32, name="acc_out", tag=f"bank{(5 + n) % 8}")
+        def second_product(n, acc):
+            a, b = (EIGHTH * e for e in END_PIECES[n])
             z_codes = keep.tile([P, b - a], U32, name=f"z_codes{n}", align_bytes=64)
             z_bytes = keep.tile([P, b - a], U8, name=f"z_bytes{n}", align_bytes=64)
             nc.vector.quantize_mx(
@@ -183,7 +197,7 @@ def tile_picked_hub_relu_e_kernel(
                 in_=z_rounded[n][:].rearrange("p w j -> p (w j)"),
             )
             nc.tensor.matmul_mx(
-                out=acc_out[n][:],
+                out=acc,
                 lhsT=w3_codes[:].bitcast(FP8X4),
                 lhsT_scale=w3_bytes[:],
                 rhs=z_codes[:].bitcast(FP8X4),
@@ -192,58 +206,62 @@ def tile_picked_hub_relu_e_kernel(
                 stop=True,
             )
 
-        def store(n, copy):
-            a, b = END_PIECES[n]
-            result = keep.tile([P, b - a], F32, name=f"result{n}")
-            copy(out=result[:], in_=acc_out[n][:])
-            nc.sync.dma_start(out=out[:, a:b], in_=result[:])
+        def store(a, acc, copy):
+            result = keep.tile(acc.shape, F32, name=f"result{a}")
+            copy(out=result[:], in_=acc)
+            nc.sync.dma_start(out=out[:, a : a + acc.shape[1]], in_=result[:])
 
-        round_weight(0, 0, scalar)
-        quantise_weight(0, 0)
-        round_weight(0, 1, vector)
+        quantise_picked(1)
+        round_weight(0, 0, vector, "woven0")
+        quantise_weight(0, (0, 1), "w_codes00")
+        x_codes[1] = keep.tile([P, HALF], U32, name="x_codes1", tag="woven0", align_bytes=64)
+        quantise_picked(2)
+        quantise_picked(3)
+        round_weight(0, 1, scalar, "w_bf01")
         for q in range(4):
-            first_product(0, 0, q * QUARTER, (q + 1) * QUARTER, vector if q == 2 else scalar)
-        fetch_source(0, 0, on_scalar)
-        round_weight(1, 0, vector)
-        quantise_weight(0, 1)
-        products(0, 1, vector, scalar)
-        quantise_weight(1, 0)
-        fetch_source(1, 0, on_scalar)
-        round_weight(1, 1, vector)
-        products(1, 0, vector, vector)
-        quantise_weight(1, 1)
-        add_target(0, 0, HALF)
-        products(0, 2, scalar, scalar)
-        products(1, 1, scalar, scalar)
-        products(1, 3, vector, vector)
-        fetch_source(2, 0, on_scalar)
-        add_target(1, 0, HALF)
-        products(1, 2, scalar, scalar)
-        fetch_source(0, 1, on_vector)
-        products(0, 3, scalar, scalar)
-        add_target(2, 0, HALF)
-        fetch_source(3, 0, on_scalar)
-        add_target(0, HALF, S)
-        fetch_source(1, 1, on_scalar)
-        add_target(3, 0, HALF)
-        fetch_source(2, 1, on_scalar)
-        add_target(1, HALF, S)
-        fetch_source(3, 1, on_scalar)
-        add_target(2, HALF, S)
-        rectify(0, True)
-        rectify(1, True)
-        for n in (2, 3, 4):
-            add_target(3, *END_PIECES[n])
-        second_product(0)
-        store(0, scalar)
-        rectify(2, False)
-        second_product(1)
-        store(1, scalar)
-        rectify(3, False)
-        second_product(2)
-        store(2, scalar)
-        rectify(4, False)
-        second_product(3)
-        store(3, scalar)
-        second_product(4)
-        store(4, vector)
+            first_product(0, 0, q * QUARTER, (q + 1) * QUARTER, scalar if q else vector, q)
+        round_weight(1, 0, vector, "woven2")
+        round_weight(1, 1, vector, "woven3")
+        products(0, 1, scalar, scalar, (1, 4))
+        fetch_target(0, 0, S, 0)
+        quantise_weight(1, (0, 1), "w_codes10")
+        quantise_weight(1, (2, 3), "w_codes12")
+        products(1, 0, vector, vector, (6, 7))
+        quantise_weight(0, (2, 3), "woven2")
+        fetch_target(1, 0, HALF, 1)
+        products(0, 2, scalar, scalar, (0, 2))
+        products(1, 1, vector, vector, (3, 5))
+        fetch_target(2, 0, HALF, 2)
+        add_source(0, 0, S)
+        add_source(1, 0, HALF)
+        products(1, 2, vector, scalar, (4, 1))
+        products(1, 3, vector, vector, (6, 7))
+        add_source(2, 0, HALF)
+        products(0, 3, scalar, scalar, (0, 2))
+        fetch_target(3, 0, HALF, 3)
+        add_source(3, 0, HALF)
+        for t in (1, 2, 3):
+            fetch_target(t, HALF, S, 3)
+        add_source(1, HALF, S)
+        add_source(2, HALF, S)
+        rectify(0, QUARTER)
+        rectify(1, EIGHTH)
+        rectify(2, EIGHTH)
+        add_source(3, HALF + EIGHTH, S - EIGHTH)
+        add_source(3, HALF, HALF + EIGHTH)
+        rectify(3, 0)
+        add_source(3, S - EIGHTH, S)
+        rectify(4, EIGHTH)
+        for n in (0, 3, 1, 5):
+            a, b = (EIGHTH * e for e in END_PIECES[n])
+            acc_out[n] = psum.tile([P, b - a], F32, name="acc_out", tag=f"bank{n}")
+        last = psum.tile([P, QUARTER], F32, name="acc_out", tag="bank2")
+        second_product(0, acc_out[0][:])
+        rectify(5, 0)
+        for n in (3, 1, 5):
+            second_product(n, acc_out[n][:])
+        second_product(2, last[:, :EIGHTH])
+        second_product(4, last[:, EIGHTH:])
+        for n in (0, 3, 1, 5):
+            store(EIGHTH * END_PIECES[n][0], acc_out[n][:], scalar)
+        store(HALF - EIGHTH, last[:], vector)

@@ -251,7 +251,7 @@ def tile_picked_hub_relu_e_kernel(
         add_source(3, HALF, HALF + EIGHTH)
         rectify(3, 0)
         add_source(3, S - EIGHTH, S)
-        rectify(4, EIGHTH)
+        rectify(4, 0)
         for n in (0, 3, 1, 5):
             a, b = (EIGHTH * e for e in END_PIECES[n])
             acc_out[n] = psum.tile([P, b - a], F32, name="acc_out", tag=f"bank{n}")

@@ -21,7 +21,7 @@ EIGHTH = S // 8
 FLOPS = 2 * (2 * K * H * S + H * N * S)
 
 
-END_PIECES = ((0, 2), (2, 3), (3, 4), (5, 7), (4, 5), (7, 8))
+END_PIECES = ((0, 2), (2, 4), (4, 5), (5, 6), (6, 7), (7, 8))
 
 
 def interleaved(view):
@@ -102,36 +102,38 @@ def tile_picked_hub_relu_e_kernel(
         for j in range(PACK - 1):
             for q in range(4):
                 look_up(j, q, on_vector if q < PACK - 1 - j else on_scalar, picked[q][:, j, :])
-        def weave(q, planes, copy):
-            copy(interleaved(woven[q][:, :, :planes]), stacked(picked[q][:, :planes, :]))
+        def weave(q, planes, copy, a, b):
+            copy(interleaved(woven[q][:, a:b, :planes]), stacked(picked[q][:, :planes, a:b]))
 
-        for q in range(3):
-            weave(q, PACK - 1, nc.vector.tensor_copy)
+        inserted = {0: QUARTER, 1: QUARTER, 2: EIGHTH}
+        for q, width in inserted.items():
+            weave(q, PACK - 1, nc.vector.tensor_copy, 0, width)
         look_up(PACK - 1, 0, on_vector, woven[0][:, :, PACK - 1])
         for q in range(1, 4):
             look_up(PACK - 1, q, on_scalar, picked[q][:, PACK - 1, :])
             if q < 3:
-                nc.vector.tensor_copy(woven[q][:, :, PACK - 1], picked[q][:, PACK - 1, :])
+                nc.vector.tensor_copy(woven[q][:, : inserted[q], PACK - 1], picked[q][:, PACK - 1, : inserted[q]])
         quantise_picked(0)
-        weave(3, PACK, nc.scalar.copy)
+        weave(2, PACK, nc.scalar.copy, EIGHTH, QUARTER)
+        weave(3, PACK, nc.scalar.copy, 0, QUARTER)
 
         w_rounded, w_codes, w_bytes = {}, {}, {}
 
-        def round_weight(i, g, copy, tag):
-            w_rounded[i, g] = keep.tile([P, 2, P, PACK], BF16, name=f"w_bf{i}{g}", tag=tag, align_bytes=64)
-            copy(
-                out=w_rounded[i, g][:].rearrange("p t m j -> p m j t"),
-                in_=w_raw[i][:].rearrange("p (j m t) -> p m j t", j=PACK, t=PACK)[:, :, :, 2 * g : 2 * g + 2],
-            )
+        def round_weight(i, g, copies, tile):
+            w_rounded[i, g] = tile
+            into = tile[:].rearrange("p t m j -> p m j t")
+            values = w_raw[i][:].rearrange("p (j m t) -> p m j t", j=PACK, t=PACK)[:, :, :, 2 * g : 2 * g + 2]
+            share = P // len(copies)
+            for n, copy in enumerate(copies):
+                copy(out=into[:, n * share : (n + 1) * share], in_=values[:, n * share : (n + 1) * share])
 
-        def quantise_weight(i, tiles, tag):
+        def quantise_weight(i, tiles, values, tag):
             codes = keep.tile([P, len(tiles) * P], U32, name=f"w_codes{i}{tiles[0]}", tag=tag, align_bytes=64)
             scales = keep.tile([P, len(tiles) * P], U8, name=f"w_bytes{i}{tiles[0]}", align_bytes=64)
-            g, first = divmod(tiles[0], 2)
             nc.vector.quantize_mx(
                 out=codes[:].bitcast(FP8X4),
                 scales=scales[:],
-                in_=w_rounded[i, g][:, first : first + len(tiles)].rearrange("p t m j -> p (t m j)"),
+                in_=values.rearrange("p t m j -> p (t m j)"),
             )
             for n, t in enumerate(tiles):
                 w_codes[i, t] = codes[:, n * P : (n + 1) * P]
@@ -161,8 +163,9 @@ def tile_picked_hub_relu_e_kernel(
             first_product(i, t, HALF, S, second, banks[1])
 
         scalar, vector = nc.scalar.copy, nc.vector.tensor_copy
+
         fetched = keep.tile([P, PACK, S], F32, name="fetched")
-        sums = keep.tile([P, PACK, S], F32, name="sums")
+        sums = [keep.tile([P, PACK, HALF], F32, name=f"sums{h}") for h in range(2)]
 
         def fetch_target(t, a, b, upto):
             window = targets[:, (t - 1) * S : upto * S] if t else parts[0][0]
@@ -170,7 +173,7 @@ def tile_picked_hub_relu_e_kernel(
 
         def add_source(t, a, b):
             nc.vector.tensor_tensor(
-                sums[:, t, a:b], parts[1][t].indirect(entries(src_sb, a, b)), fetched[:, t, a:b], ALU.add
+                sums[a // HALF][:, t, a % HALF : a % HALF + b - a], parts[1][t].indirect(entries(src_sb, a, b)), fetched[:, t, a:b], ALU.add
             )
 
         z_rounded, acc_out = {}, {}
@@ -178,13 +181,14 @@ def tile_picked_hub_relu_e_kernel(
         def rectify(n, share):
             a, b = (EIGHTH * e for e in END_PIECES[n])
             z_rounded[n] = keep.tile([P, b - a, PACK], BF16, name=f"z_bf{n}", align_bytes=64)
+            values = sums[a // HALF][:, :, a % HALF : a % HALF + b - a]
             if share:
                 nc.scalar.activation(
-                    out=interleaved(z_rounded[n][:, :share]), in_=stacked(sums[:, :, a : a + share]), func=ACT.Relu
+                    out=interleaved(z_rounded[n][:, :share]), in_=stacked(values[:, :, :share]), func=ACT.Relu
                 )
             if share < b - a:
                 nc.vector.tensor_scalar_max(
-                    interleaved(z_rounded[n][:, share:]), stacked(sums[:, :, a + share : b]), 0.0
+                    interleaved(z_rounded[n][:, share:]), stacked(values[:, :, share:]), 0.0
                 )
 
         def second_product(n, acc):
@@ -206,62 +210,67 @@ def tile_picked_hub_relu_e_kernel(
                 stop=True,
             )
 
-        def store(a, acc, copy):
-            result = keep.tile(acc.shape, F32, name=f"result{a}")
+        def store(a, acc, copy, tag):
+            result = keep.tile(acc.shape, F32, name=f"result{a}", tag=tag, align_bytes=64)
             copy(out=result[:], in_=acc)
             nc.sync.dma_start(out=out[:, a : a + acc.shape[1]], in_=result[:])
 
         quantise_picked(1)
-        round_weight(0, 0, vector, "woven0")
-        quantise_weight(0, (0, 1), "w_codes00")
+        round_weight(0, 0, [vector], keep.tile([P, 2, P, PACK], BF16, name="w_bf00", tag="woven0", align_bytes=64))
+        quantise_weight(0, (0, 1), w_rounded[0, 0][:], "w_codes00")
         x_codes[1] = keep.tile([P, HALF], U32, name="x_codes1", tag="woven0", align_bytes=64)
         quantise_picked(2)
         quantise_picked(3)
-        round_weight(0, 1, scalar, "w_bf01")
+        round_weight(0, 1, [vector, vector], keep.tile([P, 2, P, PACK], BF16, name="w_bf01", align_bytes=64))
         for q in range(4):
-            first_product(0, 0, q * QUARTER, (q + 1) * QUARTER, scalar if q else vector, q)
-        round_weight(1, 0, vector, "woven2")
-        round_weight(1, 1, vector, "woven3")
+            first_product(0, 0, q * QUARTER, (q + 1) * QUARTER, scalar, q)
+        quantise_weight(0, (2, 3), w_rounded[0, 1][:], "woven3")
+        round_weight(1, 0, [vector], keep.tile([P, 2, P, PACK], BF16, name="w_bf10", tag="woven2", align_bytes=64))
+        round_weight(1, 1, [vector], keep.tile([P, 2, P, PACK], BF16, name="w_bf11", tag="woven1", align_bytes=64))
         products(0, 1, scalar, scalar, (1, 4))
         fetch_target(0, 0, S, 0)
-        quantise_weight(1, (0, 1), "w_codes10")
-        quantise_weight(1, (2, 3), "w_codes12")
+        quantise_weight(1, (0,), w_rounded[1, 0][:, :1], "w_codes10")
+        quantise_weight(1, (2, 3), w_rounded[1, 1][:], "w_codes12")
+        quantise_weight(1, (1,), w_rounded[1, 0][:, 1:], "w_codes11")
         products(1, 0, vector, vector, (6, 7))
-        quantise_weight(0, (2, 3), "woven2")
         fetch_target(1, 0, HALF, 1)
-        products(0, 2, scalar, scalar, (0, 2))
         products(1, 1, vector, vector, (3, 5))
+        products(1, 2, vector, vector, (4, 1))
+        products(0, 2, scalar, scalar, (6, 7))
+        first_product(1, 3, 0, HALF, vector, 0)
         fetch_target(2, 0, HALF, 2)
-        add_source(0, 0, S)
+        add_source(0, 0, HALF)
+        add_source(0, HALF, S)
         add_source(1, 0, HALF)
-        products(1, 2, vector, scalar, (4, 1))
-        products(1, 3, vector, vector, (6, 7))
         add_source(2, 0, HALF)
-        products(0, 3, scalar, scalar, (0, 2))
+        products(0, 3, scalar, scalar, (3, 5))
+        first_product(1, 3, HALF, S, scalar, 6)
         fetch_target(3, 0, HALF, 3)
         add_source(3, 0, HALF)
         for t in (1, 2, 3):
             fetch_target(t, HALF, S, 3)
+        rectify(1, 0)
         add_source(1, HALF, S)
         add_source(2, HALF, S)
         rectify(0, QUARTER)
-        rectify(1, EIGHTH)
-        rectify(2, EIGHTH)
-        add_source(3, HALF + EIGHTH, S - EIGHTH)
-        add_source(3, HALF, HALF + EIGHTH)
-        rectify(3, 0)
-        add_source(3, S - EIGHTH, S)
-        rectify(4, 0)
-        for n in (0, 3, 1, 5):
-            a, b = (EIGHTH * e for e in END_PIECES[n])
-            acc_out[n] = psum.tile([P, b - a], F32, name="acc_out", tag=f"bank{n}")
-        last = psum.tile([P, QUARTER], F32, name="acc_out", tag="bank2")
-        second_product(0, acc_out[0][:])
-        rectify(5, 0)
-        for n in (3, 1, 5):
+        for n in (1, 0):
+            acc_out[n] = psum.tile([P, QUARTER], F32, name="acc_out", tag=f"bank{n}")
             second_product(n, acc_out[n][:])
-        second_product(2, last[:, :EIGHTH])
-        second_product(4, last[:, EIGHTH:])
-        for n in (0, 3, 1, 5):
-            store(EIGHTH * END_PIECES[n][0], acc_out[n][:], scalar)
-        store(HALF - EIGHTH, last[:], vector)
+        early = keep.tile([P, HALF], F32, name="early", tag="targets")
+        for n in (1, 0):
+            cols = slice(n * QUARTER, (n + 1) * QUARTER)
+            scalar(out=early[:, cols], in_=acc_out[n][:])
+            nc.sync.dma_start(out=out[:, cols], in_=early[:, cols])
+        for n in (2, 3, 4, 5):
+            add_source(3, *(EIGHTH * e for e in END_PIECES[n]))
+        rectify(2, EIGHTH)
+        rectify(3, EIGHTH)
+        rectify(4, 0)
+        rectify(5, 0)
+        for n in (2, 4, 5, 3):
+            acc_out[n] = psum.tile([P, EIGHTH], F32, name="acc_out", tag=f"bank{n}")
+            second_product(n, acc_out[n][:])
+        for n in (2, 4):
+            store(EIGHTH * END_PIECES[n][0], acc_out[n][:], scalar, f"result{n}")
+        store(EIGHTH * END_PIECES[5][0], acc_out[5][:], vector, "z_bf3")
+        store(EIGHTH * END_PIECES[3][0], acc_out[3][:], vector, "result3")

@@ -42,6 +42,7 @@ def tile_picked_hub_relu_e_kernel(
     nc = tc.nc
     with ExitStack() as ctx:
         keep = ctx.enter_context(tc.tile_pool(name="keep", bufs=1))
+        shared = ctx.enter_context(tc.tile_pool(name="shared", bufs=1))
         psum = ctx.enter_context(tc.psum_pool(name="psum", bufs=1))
 
         offs_sb = keep.tile([P, S // 16], U16, name="offs_sb")
@@ -61,11 +62,12 @@ def tile_picked_hub_relu_e_kernel(
                 nc.sync.dma_start(offs_sb[:], offs)
         w_raw = []
         for i, w in enumerate((w2, w1)):
-            raw = keep.tile([P, PACK * H], F32, name=f"w_raw{i}")
+            raw = keep.tile([P, PACK * H], F32, name=f"w_raw{i}", align_bytes=64)
             nc.sync.dma_start(out=raw[:], in_=w.rearrange("(p j) c -> p (j c)", j=PACK))
             w_raw.append(raw)
+            if i == 0:
+                nc.sync.dma_start(dst_sb[:], dst)
         nc.sync.dma_start(src_sb[:], src)
-        nc.sync.dma_start(dst_sb[:], dst)
         nc.sync.dma_start(
             out=w3_codes[:].bitcast(I32),
             in_=w3_words[0].rearrange("p n t -> p (n t)").bitcast(I32),
@@ -139,9 +141,8 @@ def tile_picked_hub_relu_e_kernel(
                 w_codes[i, t] = codes[:, n * P : (n + 1) * P]
                 w_bytes[i, t] = scales[:, n * P : (n + 1) * P]
 
-        targets = keep.tile([P, (PACK - 1) * S], F32, name="targets")
         parts = [
-            [x_raw[0][:]] + [targets[:, t * S : (t + 1) * S] for t in range(PACK - 1)],
+            [x_raw[0][:], None] + [keep.tile([P, S], F32, name=f"targets{t}")[:] for t in (2, 3)],
             [x_raw[1][:]] + [keep.tile([P, S], F32, name=f"sources{t}")[:] for t in range(1, PACK)],
         ]
 
@@ -164,16 +165,18 @@ def tile_picked_hub_relu_e_kernel(
 
         scalar, vector = nc.scalar.copy, nc.vector.tensor_copy
 
-        fetched = keep.tile([P, PACK, S], F32, name="fetched")
-        sums = [keep.tile([P, PACK, HALF], F32, name=f"sums{h}") for h in range(2)]
+        fetched = {}
+        sums = {}
 
-        def fetch_target(t, a, b, upto):
-            window = targets[:, (t - 1) * S : upto * S] if t else parts[0][0]
-            on_scalar(fetched[:, t, a:b], window, entries(dst_sb, a, b))
+        def fetch_target(t, a, b, tag):
+            tile = keep.tile([P, b - a], F32, name=f"fetched{t}_{a}", tag=tag, align_bytes=64)
+            on_scalar(tile[:], parts[0][t], entries(dst_sb, a, b))
+            for h in range(a // HALF, b // HALF):
+                fetched[t, h] = tile[:, h * HALF - a : (h + 1) * HALF - a]
 
         def add_source(t, a, b):
             nc.vector.tensor_tensor(
-                sums[a // HALF][:, t, a % HALF : a % HALF + b - a], parts[1][t].indirect(entries(src_sb, a, b)), fetched[:, t, a:b], ALU.add
+                sums[a // HALF][:, t, a % HALF : a % HALF + b - a], parts[1][t].indirect(entries(src_sb, a, b)), fetched[t, a // HALF][:, a % HALF : a % HALF + b - a], ALU.add
             )
 
         z_rounded, acc_out = {}, {}
@@ -225,30 +228,37 @@ def tile_picked_hub_relu_e_kernel(
         for q in range(4):
             first_product(0, 0, q * QUARTER, (q + 1) * QUARTER, scalar, q)
         quantise_weight(0, (2, 3), w_rounded[0, 1][:], "woven3")
-        round_weight(1, 0, [vector], keep.tile([P, 2, P, PACK], BF16, name="w_bf10", tag="woven2", align_bytes=64))
-        round_weight(1, 1, [vector], keep.tile([P, 2, P, PACK], BF16, name="w_bf11", tag="woven1", align_bytes=64))
-        products(0, 1, scalar, scalar, (1, 4))
-        fetch_target(0, 0, S, 0)
-        quantise_weight(1, (0,), w_rounded[1, 0][:, :1], "w_codes10")
-        quantise_weight(1, (2, 3), w_rounded[1, 1][:], "w_codes12")
-        quantise_weight(1, (1,), w_rounded[1, 0][:, 1:], "w_codes11")
-        products(1, 0, vector, vector, (6, 7))
-        fetch_target(1, 0, HALF, 1)
-        products(1, 1, vector, vector, (3, 5))
-        products(1, 2, vector, vector, (4, 1))
-        products(0, 2, scalar, scalar, (6, 7))
-        first_product(1, 3, 0, HALF, vector, 0)
-        fetch_target(2, 0, HALF, 2)
-        add_source(0, 0, HALF)
+        round_weight(1, 0, [vector], shared.tile([P, 2, P, PACK], BF16, name="w_bf10", offset=3072, align_bytes=64))
+        first_product(0, 2, HALF, S, scalar, 4)
+        fetch_target(0, 0, S, "fetched0")
+        quantise_weight(1, (0, 1), w_rounded[1, 0][:], "w_codes10")
+        late = shared.tile([P, 2, P, PACK], BF16, name="w_bf11", offset=4096, align_bytes=64)
+        nc.gpsimd.tensor_scalar(
+            late[:], w_raw[1][:].rearrange("p (j m t) -> p t m j", j=PACK, t=PACK)[:, 2:], 1.0, 0.0, ALU.mult, ALU.add
+        )
+        parts[0][1] = shared.tile([P, S], F32, name="targets1", offset=0, align_bytes=64)[:]
+        products(0, 1, vector, vector, (1, 6))
+        fetch_target(1, 0, HALF, "fetched1")
+        products(1, 0, vector, vector, (7, 0))
+        first_product(0, 2, 0, HALF, vector, 1)
+        first_product(1, 1, 0, QUARTER, vector, 5)
+        first_product(1, 1, QUARTER, HALF, scalar, 3)
+        first_product(1, 1, HALF, S, scalar, 2)
+        fetch_target(2, 0, HALF, "fetched2")
+        products(0, 3, vector, vector, (6, 7))
+        quantise_weight(1, (2, 3), late[:], "w_codes12")
+        sums[0] = shared.tile([P, PACK, HALF], F32, name="sums0", offset=4096, align_bytes=64)
+        sums[1] = keep.tile([P, PACK, HALF], F32, name="sums1", tag="w_raw1", align_bytes=64)
         add_source(0, HALF, S)
+        add_source(0, 0, HALF)
         add_source(1, 0, HALF)
+        products(1, 2, scalar, scalar, (3, 4))
+        fetch_target(3, 0, HALF, "fetched3")
+        products(1, 3, scalar, scalar, (0, 1))
         add_source(2, 0, HALF)
-        products(0, 3, scalar, scalar, (3, 5))
-        first_product(1, 3, HALF, S, scalar, 6)
-        fetch_target(3, 0, HALF, 3)
         add_source(3, 0, HALF)
-        for t in (1, 2, 3):
-            fetch_target(t, HALF, S, 3)
+        for t, tag in ((1, "x_bytes"), (2, "woven0"), (3, "w_codes12")):
+            fetch_target(t, HALF, S, tag)
         rectify(1, 0)
         add_source(1, HALF, S)
         add_source(2, HALF, S)
@@ -256,7 +266,7 @@ def tile_picked_hub_relu_e_kernel(
         for n in (1, 0):
             acc_out[n] = psum.tile([P, QUARTER], F32, name="acc_out", tag=f"bank{n}")
             second_product(n, acc_out[n][:])
-        early = keep.tile([P, HALF], F32, name="early", tag="targets")
+        early = keep.tile([P, HALF], F32, name="early", tag="targets3")
         for n in (1, 0):
             cols = slice(n * QUARTER, (n + 1) * QUARTER)
             scalar(out=early[:, cols], in_=acc_out[n][:])

from contextlib import ExitStack

import concourse.mybir as mybir

F32 = mybir.dt.float32
BF16 = mybir.dt.bfloat16
I32 = mybir.dt.int32
U32 = mybir.dt.uint32
U16 = mybir.dt.uint16
U8 = mybir.dt.uint8
FP8X4 = mybir.dt.float8_e4m3fn_x4
ACT = mybir.ActivationFunctionType
ALU = mybir.AluOpType

K, T, S, H, N = 512, 2048, 1024, 512, 128
P = 128
PACK = 4
HALF = S // 2
QUARTER = S // 4
EIGHTH = S // 8
FLOPS = 2 * (2 * K * H * S + H * N * S)


END_PIECES = ((0, 2), (2, 4), (4, 5), (5, 6), (6, 7), (7, 8))


def interleaved(view):
    return view.rearrange("p (c i) t -> p c t i", i=4)


def stacked(view):
    return view.rearrange("p t (c i) -> p c t i", i=4)


def entries(offsets, a, b):
    return offsets[:, a // 16 : b // 16]


def tile_picked_hub_relu_e_kernel(
    tc, xT, w1, w2, w3_words, w3_scales, offs, src, dst, out
):
    nc = tc.nc
    with ExitStack() as ctx:
        keep = ctx.enter_context(tc.tile_pool(name="keep", bufs=1))
        shared = ctx.enter_context(tc.tile_pool(name="shared", bufs=1))
        psum = ctx.enter_context(tc.psum_pool(name="psum", bufs=1))

        offs_sb = keep.tile([P, S // 16], U16, name="offs_sb")
        src_sb = keep.tile([P, S // 16], U16, name="src_sb")
        dst_sb = keep.tile([P, S // 16], U16, name="dst_sb")

        w3_codes = keep.tile([P, N], U32, name="w3_codes", align_bytes=64)
        w3_bytes = keep.tile([P, N], U8, name="w3_bytes", align_bytes=64)
        nc.vector.memset(w3_bytes[:].bitcast(I32), 0)

        x_view = xT.rearrange("(p j) n -> p j n", j=PACK)
        x_raw = []
        for j in range(PACK):
            x_raw.append(keep.tile([P, T], F32, name=f"x_raw{j}"))
            nc.sync.dma_start(out=x_raw[j][:], in_=x_view[:, j, :])
            if j == 0:
                nc.sync.dma_start(offs_sb[:], offs)
        w_raw = []
        for i, w in enumerate((w2, w1)):
            raw = keep.tile([P, PACK * H], F32, name=f"w_raw{i}", align_bytes=64)
            nc.sync.dma_start(out=raw[:], in_=w.rearrange("(p j) c -> p (j c)", j=PACK))
            w_raw.append(raw)
            if i == 0:
                nc.sync.dma_start(dst_sb[:], dst)
        nc.sync.dma_start(src_sb[:], src)
        nc.sync.dma_start(
            out=w3_codes[:].bitcast(I32),
            in_=w3_words[0].rearrange("p n t -> p (n t)").bitcast(I32),
        )
        for q in range(4):
            nc.sync.dma_start(
                out=w3_bytes[32 * q : 32 * q + 4, :].bitcast(I32),
                in_=w3_scales[0, 4 * q : 4 * q + 4, :].bitcast(I32),
            )

        def on_scalar(into, window, offsets):
            nc.scalar.activation(out=into, in_=window.indirect(offsets), func=ACT.Copy)

        def on_vector(into, window, offsets):
            nc.vector.tensor_copy(into, window.indirect(offsets))

        woven = [keep.tile([P, QUARTER, PACK], BF16, name=f"woven{q}", align_bytes=64) for q in range(4)]
        x_codes = {0: keep.tile([P, HALF], U32, name="x_codes0", align_bytes=64)}
        x_bytes = keep.tile([P, S], U8, name="x_bytes", align_bytes=64)

        def quantise_picked(q):
            cols = slice(q * QUARTER, (q + 1) * QUARTER)
            nc.vector.quantize_mx(
                out=x_codes[q // 2][:, (q % 2) * QUARTER : (q % 2 + 1) * QUARTER].bitcast(FP8X4),
                scales=x_bytes[:, cols],
                in_=woven[q][:].rearrange("p c j -> p (c j)"),
            )

        picked = [keep.tile([P, PACK, QUARTER], BF16, name=f"picked{q}") for q in range(4)]

        def look_up(j, q, gather, into):
            gather(into, x_raw[j][:], entries(offs_sb, q * QUARTER, (q + 1) * QUARTER))

        for j in range(PACK - 1):
            for q in range(4):
                look_up(j, q, on_vector if q < PACK - 1 - j else on_scalar, picked[q][:, j, :])
        def weave(q, planes, copy, a, b):
            copy(interleaved(woven[q][:, a:b, :planes]), stacked(picked[q][:, :planes, a:b]))

        inserted = {0: QUARTER, 1: QUARTER, 2: EIGHTH}
        for q, width in inserted.items():
            weave(q, PACK - 1, nc.vector.tensor_copy, 0, width)
        look_up(PACK - 1, 0, on_vector, woven[0][:, :, PACK - 1])
        for q in range(1, 4):
            look_up(PACK - 1, q, on_scalar, picked[q][:, PACK - 1, :])
            if q < 3:
                nc.vector.tensor_copy(woven[q][:, : inserted[q], PACK - 1], picked[q][:, PACK - 1, : inserted[q]])
        quantise_picked(0)
        weave(2, PACK, nc.scalar.copy, EIGHTH, QUARTER)
        weave(3, PACK, nc.scalar.copy, 0, QUARTER)

        w_rounded, w_codes, w_bytes = {}, {}, {}

        def round_weight(i, g, copies, tile):
            w_rounded[i, g] = tile
            into = tile[:].rearrange("p t m j -> p m j t")
            values = w_raw[i][:].rearrange("p (j m t) -> p m j t", j=PACK, t=PACK)[:, :, :, 2 * g : 2 * g + 2]
            share = P // len(copies)
            for n, copy in enumerate(copies):
                copy(out=into[:, n * share : (n + 1) * share], in_=values[:, n * share : (n + 1) * share])

        def quantise_weight(i, tiles, values, tag):
            codes = keep.tile([P, len(tiles) * P], U32, name=f"w_codes{i}{tiles[0]}", tag=tag, align_bytes=64)
            scales = keep.tile([P, len(tiles) * P], U8, name=f"w_bytes{i}{tiles[0]}", align_bytes=64)
            nc.vector.quantize_mx(
                out=codes[:].bitcast(FP8X4),
                scales=scales[:],
                in_=values.rearrange("p t m j -> p (t m j)"),
            )
            for n, t in enumerate(tiles):
                w_codes[i, t] = codes[:, n * P : (n + 1) * P]
                w_bytes[i, t] = scales[:, n * P : (n + 1) * P]

        parts = [
            [x_raw[0][:], None] + [keep.tile([P, S], F32, name=f"targets{t}")[:] for t in (2, 3)],
            [x_raw[1][:]] + [keep.tile([P, S], F32, name=f"sources{t}")[:] for t in range(1, PACK)],
        ]

        def first_product(i, t, a, b, copy, bank):
            acc = psum.tile([P, b - a], F32, name="acc", tag=f"bank{bank}")
            nc.tensor.matmul_mx(
                out=acc[:],
                lhsT=w_codes[i, t].bitcast(FP8X4),
                lhsT_scale=w_bytes[i, t],
                rhs=x_codes[a // HALF][:, a % HALF : a % HALF + b - a].bitcast(FP8X4),
                rhs_scale=x_bytes[:, a:b],
                start=True,
                stop=True,
            )
            copy(out=parts[i][t][:, a:b], in_=acc[:])

        def products(i, t, first, second, banks):
            first_product(i, t, 0, HALF, first, banks[0])
            first_product(i, t, HALF, S, second, banks[1])

        scalar, vector = nc.scalar.copy, nc.vector.tensor_copy

        fetched = {}
        sums = {}

        def fetch_target(t, a, b, tag):
            tile = keep.tile([P, b - a], F32, name=f"fetched{t}_{a}", tag=tag, align_bytes=64)
            on_scalar(tile[:], parts[0][t], entries(dst_sb, a, b))
            for h in range(a // HALF, b // HALF):
                fetched[t, h] = tile[:, h * HALF - a : (h + 1) * HALF - a]

        def add_source(t, a, b):
            nc.vector.tensor_tensor(
                sums[a // HALF][:, t, a % HALF : a % HALF + b - a], parts[1][t].indirect(entries(src_sb, a, b)), fetched[t, a // HALF][:, a % HALF : a % HALF + b - a], ALU.add
            )

        z_rounded, acc_out = {}, {}

        def rectify(n, share):
            a, b = (EIGHTH * e for e in END_PIECES[n])
            z_rounded[n] = keep.tile([P, b - a, PACK], BF16, name=f"z_bf{n}", align_bytes=64)
            values = sums[a // HALF][:, :, a % HALF : a % HALF + b - a]
            if share:
                nc.scalar.activation(
                    out=interleaved(z_rounded[n][:, :share]), in_=stacked(values[:, :, :share]), func=ACT.Relu
                )
            if share < b - a:
                nc.vector.tensor_scalar_max(
                    interleaved(z_rounded[n][:, share:]), stacked(values[:, :, share:]), 0.0
                )

        def second_product(n, acc):
            a, b = (EIGHTH * e for e in END_PIECES[n])
            z_codes = keep.tile([P, b - a], U32, name=f"z_codes{n}", align_bytes=64)
            z_bytes = keep.tile([P, b - a], U8, name=f"z_bytes{n}", align_bytes=64)
            nc.vector.quantize_mx(
                out=z_codes[:].bitcast(FP8X4),
                scales=z_bytes[:],
                in_=z_rounded[n][:].rearrange("p w j -> p (w j)"),
            )
            nc.tensor.matmul_mx(
                out=acc,
                lhsT=w3_codes[:].bitcast(FP8X4),
                lhsT_scale=w3_bytes[:],
                rhs=z_codes[:].bitcast(FP8X4),
                rhs_scale=z_bytes[:],
                start=True,
                stop=True,
            )

        def store(a, acc, copy, tag):
            result = keep.tile(acc.shape, F32, name=f"result{a}", tag=tag, align_bytes=64)
            copy(out=result[:], in_=acc)
            nc.sync.dma_start(out=out[:, a : a + acc.shape[1]], in_=result[:])

        quantise_picked(1)
        round_weight(0, 0, [vector], keep.tile([P, 2, P, PACK], BF16, name="w_bf00", tag="woven0", align_bytes=64))
        quantise_weight(0, (0, 1), w_rounded[0, 0][:], "w_codes00")
        x_codes[1] = keep.tile([P, HALF], U32, name="x_codes1", tag="woven0", align_bytes=64)
        quantise_picked(2)
        quantise_picked(3)
        round_weight(0, 1, [vector, vector], keep.tile([P, 2, P, PACK], BF16, name="w_bf01", align_bytes=64))
        for q in range(4):
            first_product(0, 0, q * QUARTER, (q + 1) * QUARTER, scalar, q)
        quantise_weight(0, (2, 3), w_rounded[0, 1][:], "woven3")
        round_weight(1, 0, [vector], shared.tile([P, 2, P, PACK], BF16, name="w_bf10", offset=3072, align_bytes=64))
        first_product(0, 2, HALF, S, scalar, 4)
        fetch_target(0, 0, S, "fetched0")
        quantise_weight(1, (0, 1), w_rounded[1, 0][:], "w_codes10")
        late = shared.tile([P, 2, P, PACK], BF16, name="w_bf11", offset=4096, align_bytes=64)
        nc.gpsimd.tensor_scalar(
            late[:], w_raw[1][:].rearrange("p (j m t) -> p t m j", j=PACK, t=PACK)[:, 2:], 1.0, 0.0, ALU.mult, ALU.add
        )
        parts[0][1] = shared.tile([P, S], F32, name="targets1", offset=0, align_bytes=64)[:]
        products(0, 1, vector, vector, (1, 6))
        fetch_target(1, 0, HALF, "fetched1")
        products(1, 0, vector, vector, (7, 0))
        first_product(0, 2, 0, HALF, vector, 1)
        first_product(1, 1, 0, QUARTER, vector, 5)
        first_product(1, 1, QUARTER, HALF, scalar, 3)
        first_product(1, 1, HALF, S, scalar, 2)
        fetch_target(2, 0, HALF, "fetched2")
        products(0, 3, vector, vector, (6, 7))
        quantise_weight(1, (2, 3), late[:], "w_codes12")
        sums[0] = shared.tile([P, PACK, HALF], F32, name="sums0", offset=4096, align_bytes=64)
        sums[1] = keep.tile([P, PACK, HALF], F32, name="sums1", tag="w_raw1", align_bytes=64)
        add_source(0, HALF, S)
        add_source(0, 0, HALF)
        add_source(1, 0, HALF)
        products(1, 2, scalar, scalar, (3, 4))
        fetch_target(3, 0, HALF, "fetched3")
        products(1, 3, scalar, scalar, (0, 1))
        add_source(2, 0, HALF)
        add_source(3, 0, HALF)
        for t, tag in ((1, "x_bytes"), (2, "woven0"), (3, "w_codes12")):
            fetch_target(t, HALF, S, tag)
        rectify(1, 0)
        add_source(1, HALF, S)
        add_source(2, HALF, S)
        rectify(0, QUARTER)
        for n in (1, 0):
            acc_out[n] = psum.tile([P, QUARTER], F32, name="acc_out", tag=f"bank{n}")
            second_product(n, acc_out[n][:])
        early = keep.tile([P, HALF], F32, name="early", tag="targets3")
        for n in (1, 0):
            cols = slice(n * QUARTER, (n + 1) * QUARTER)
            scalar(out=early[:, cols], in_=acc_out[n][:])
            nc.sync.dma_start(out=out[:, cols], in_=early[:, cols])
        for n in (2, 3, 4, 5):
            add_source(3, *(EIGHTH * e for e in END_PIECES[n]))
        rectify(2, EIGHTH)
        rectify(3, EIGHTH)
        rectify(4, 0)
        rectify(5, 0)
        for n in (2, 4, 5, 3):
            acc_out[n] = psum.tile([P, EIGHTH], F32, name="acc_out", tag=f"bank{n}")
            second_product(n, acc_out[n][:])
        for n in (2, 4):
            store(EIGHTH * END_PIECES[n][0], acc_out[n][:], scalar, f"result{n}")
        store(EIGHTH * END_PIECES[5][0], acc_out[5][:], vector, "z_bf3")
        store(EIGHTH * END_PIECES[3][0], acc_out[3][:], vector, "result3")
